import numpy as np
import ml_dtypes


def mxq(x, axis, fmt="e4m3"):
    dtype, down = {"e4m3": (ml_dtypes.float8_e4m3fn, 7), "e5m2": (ml_dtypes.float8_e5m2, 14)}[fmt]
    v = np.moveaxis(np.asarray(x, np.float32).astype(ml_dtypes.bfloat16).astype(np.float64), axis, -1)
    blocks = v.reshape(v.shape[:-1] + (-1, 32))
    amax = np.abs(blocks).max(-1, keepdims=True)
    byte = np.maximum(np.where(amax > 0, np.frexp(amax)[1] - 1 + 127, 0) - down, 1)
    scale = np.exp2(byte - 127.0)
    codes = (blocks / scale).astype(np.float32).astype(dtype).astype(np.float64)
    return np.moveaxis((codes * scale).reshape(v.shape), -1, axis)


WIDE = False


def mx_kscale(k):
    if not WIDE:
        return np.ones(k)
    levels = np.array([24, -24, 12, -12, 0])
    if k % 512:
        return np.exp2(np.random.permutation(np.resize(levels, k // 32))).repeat(32)
    a = np.empty((k // 512, 16))
    for p in range(k // 512):
        a[p, :8] = np.random.permutation(np.resize(levels, 8))
        for g in range(8):
            far = levels[np.abs(levels - a[p, g]) >= 10]
            a[p, g + 8] = far[np.random.randint(len(far))]
    return np.exp2(a.ravel()).repeat(32)


def f64(x):
    return np.asarray(x).astype(np.float64)


def striped8(idx):
    return np.concatenate([v.reshape(-1, 16).T for v in idx]).astype(np.uint16)


def unstriped8(offs):
    return np.stack([offs[16 * g:16 * g + 16].T.reshape(-1) for g in range(8)]).astype(np.int64)


E2M1 = np.array([0.0, 0.5, 1.0, 1.5, 2.0, 3.0, 4.0, 6.0, -0.0, -0.5, -1.0, -1.5, -2.0, -3.0, -4.0, -6.0])


def pack_weight(w, fmt):
    k, n = w.shape
    w = f64(np.asarray(w, np.float32).astype(ml_dtypes.bfloat16)).reshape(k // 32, 32, n)
    amax = np.abs(w).max(1)
    if fmt == "e4m3":
        byte = np.frexp(amax)[1] - 1 + 127 - 7
    else:
        mant, ex = np.frexp(amax / 6.0)
        byte = np.where(mant > 0.5, ex, ex - 1) + 127
    byte = np.clip(np.where(amax > 0, byte, 1), 1, 254)
    scaled = (w * np.exp2(127.0 - byte)[:, None, :]).reshape(k, n).astype(np.float32)
    by_word = np.ascontiguousarray(scaled.reshape(k // 512, 128, 4, n).transpose(0, 1, 3, 2))
    if fmt == "e4m3":
        words = by_word.astype(ml_dtypes.float8_e4m3fn).view(np.uint8)
    else:
        c = by_word.astype(ml_dtypes.float4_e2m1fn).view(np.uint8) & 0xF
        words = (c[..., 0::2] | (c[..., 1::2] << 4)).reshape(k // 512, 128, 2 * n)
    return np.ascontiguousarray(words), np.ascontiguousarray(byte.astype(np.uint8).reshape(k // 512, 16, n))


def unpack_weight(words, scales, fmt):
    g, _, n = scales.shape
    words = np.ascontiguousarray(words).reshape(g, 128, n, -1)
    if fmt == "e4m3":
        vals = words.view(ml_dtypes.float8_e4m3fn).astype(np.float64)
    else:
        nib = np.empty((g, 128, n, 4), np.uint8)
        nib[..., 0::2] = words & 0xF
        nib[..., 1::2] = words >> 4
        vals = E2M1[nib]
    vals = vals * np.repeat(np.exp2(scales.astype(np.float64) - 127.0), 8, axis=1)[..., None]
    return vals.transpose(0, 1, 3, 2).reshape(g * 512, n)


def gelu(f):
    return 0.5 * f * (1.0 + np.tanh(np.sqrt(2.0 / np.pi) * (f + 0.044715 * f**3)))


K, L, N, T, J = 512, 512, 512, 2048, 1024


def setup_inputs():
    n = np.random.standard_normal
    s = mx_kscale(K)[:, None]
    s2 = mx_kscale(L)[:, None]
    p_wx = pack_weight(n((L, N)) / np.sqrt(L) / s2, "e2m1")
    return {
        "xT": (n((K, T)) * s).astype(np.float32),
        "wgt": np.repeat(np.random.uniform(0.5, 2.0, (8, J)), 16, axis=0).astype(np.float32),
        "wt": (n((K, N)) / np.sqrt(K) / s).astype(np.float32),
        "c": (n((L, J)) * s2).astype(np.float32),
        "wx_words": p_wx[0],
        "wx_scales": p_wx[1],
        "b": (0.3 * n(N)).astype(np.float32),
        "offs": striped8(np.stack([np.random.permutation(T)[:J] for _ in range(8)])),
    }


def reference(xT, wgt, wt, c, wx_words, wx_scales, b, offs):
    idx = unstriped8(offs)
    rows = np.arange(K)
    xg = f64(wgt)[rows // 4 % 128] * f64(xT)[rows[:, None], idx[rows % 512 // 64]]
    xT_ = mxq(xg, 0, "e4m3")
    wt_ = mxq(f64(wt), 0, "e4m3")
    c_q_ = mxq(f64(c), 0, "e4m3")
    c_r_ = mxq(f64(c) - c_q_, 0, "e4m3")
    wx_ = unpack_weight(wx_words, wx_scales, "e2m1")
    y = wt_.T @ xT_ + wx_.T @ c_q_ + wx_.T @ c_r_
    return gelu(y + f64(b)[:, None])

@@ -1,0 +1,256 @@
+from contextlib import ExitStack
+
+import concourse.mybir as mybir
+
+K, L, N, T, J = 512, 512, 512, 2048, 1024
+FLOPS = 2 * N * J * (K + 2 * L) + 2 * L * L * J
+
+F32 = mybir.dt.float32
+BF16 = mybir.dt.bfloat16
+I32 = mybir.dt.int32
+U32 = mybir.dt.uint32
+U16 = mybir.dt.uint16
+U8 = mybir.dt.uint8
+FP8X4 = mybir.dt.float8_e4m3fn_x4
+FP4X4 = mybir.dt.float4_e2m1fn_x4
+MULT = mybir.AluOpType.mult
+SUBTRACT = mybir.AluOpType.subtract
+ADD = mybir.AluOpType.add
+IS_EQUAL = mybir.AluOpType.is_equal
+GELU = mybir.ActivationFunctionType.Gelu_apprx_tanh
+
+P = 128
+PACK = 4
+N_TILES = N // P
+BANK = 512
+UNITS = J // P
+C_WIDTHS = (128, 128, 256, 256, 256)
+X_WIDTHS = (256, 256, 256, 128, 128)
+SCALAR_LATE = ()
+
+
+def starts(widths):
+    return [sum(widths[:i]) for i in range(len(widths))]
+
+
+def woven(tile):
+    return tile.rearrange("p (c i t) -> p c t i", i=2, t=PACK)
+
+
+def planes(tile):
+    return tile.rearrange("p t (c i) -> p c t i", i=2)
+
+
+def tile_list_gelu_kernel(tc, xT, wgt, wt, c, wx_words, wx_scales, b, offs, out):
+    nc = tc.nc
+    with ExitStack() as ctx:
+        keep = ctx.enter_context(tc.tile_pool(name="keep", bufs=1))
+        psum = ctx.enter_context(tc.psum_pool(name="psum", bufs=1))
+
+        def sb(name, shape, dtype):
+            return keep.tile(shape, dtype, name=name, align_bytes=64)
+
+        def quantise(name, values, width):
+            codes = sb(name + "_codes", [P, width], U32)
+            scales = sb(name + "_scales", [P, width], U8)
+            nc.vector.quantize_mx(out=codes[:].bitcast(FP8X4), scales=scales[:], in_=values)
+            return codes, scales
+
+        ones = sb("ones", [P, P], F32)
+        nc.vector.memset(ones[:], 1.0)
+        first_row = sb("first_row", [P, 1], F32)
+        for quad in range(4):
+            nc.vector.memset(first_row[32 * quad : 32 * quad + 32, :], float(32 * quad))
+        warm = sb("warm", [P, 2], F32)
+        nc.scalar.activation(out=warm[:], in_=ones[:, 0:2], func=GELU)
+        eye = sb("eye", [P, PACK * (PACK * P + 1)], BF16)
+        nc.vector.memset(eye[:].bitcast(U32), 0)
+        counted = sb("counted", [P, 32], F32)
+        nc.vector.tensor_tensor_scan(
+            out=counted[:], data0=ones[:, 0:32], data1=ones[:, 0:32], initial=first_row[:], op0=MULT, op1=ADD
+        )
+        column = sb("column", [P, P], F32)
+        nc.vector.tensor_tensor_scan(out=column[:], data0=ones[:], data1=ones[:], initial=0.0, op0=MULT, op1=ADD)
+        row = sb("row", [P, 32], F32)
+        nc.vector.transpose(out=row[:], in_=counted[:])
+        wx_plane = sb("wx_plane", [P, N], U8)
+        nc.vector.memset(wx_plane[:].bitcast(U32), 0)
+        nc.vector.tensor_scalar(
+            out=eye[:].rearrange("p (j r) -> p j r", j=PACK)[:, :, 0 : PACK * P : PACK],
+            in0=column[:].unsqueeze(1).to_broadcast([P, PACK, P]),
+            scalar1=row[:, 0:1],
+            scalar2=None,
+            op0=IS_EQUAL,
+        )
+        eye_codes, eye_scales = quantise("eye", eye[:, 0 : PACK * PACK * P], PACK * P)
+
+        c_view = c.rearrange("(p t) j -> p t j", t=PACK)
+        c_starts = starts(C_WIDTHS)
+        c_raw = [sb("c_raw%d" % q, [P, PACK, w], F32) for q, w in enumerate(C_WIDTHS)]
+        for q, w in enumerate(C_WIDTHS):
+            nc.sync.dma_start(out=c_raw[q][:], in_=c_view[:, :, c_starts[q] : c_starts[q] + w])
+        offsets = keep.tile([P, J // 16], U16, name="offsets")
+        nc.sync.dma_start(offsets[:], offs)
+        wgt_sb = sb("wgt_sb", [P, J], F32)
+        nc.sync.dma_start(out=wgt_sb[:], in_=wgt)
+        x_view = xT.rearrange("(p t) s -> p t s", t=PACK)
+        x_sb = [sb("x_sb%d" % t, [P, T], F32) for t in range(PACK)]
+        nc.sync.dma_start(out=x_sb[0][:], in_=x_view[:, 0, :])
+        wt_raw = sb("wt_raw", [P, PACK, N], F32)
+        nc.sync.dma_start(out=wt_raw[:], in_=wt.rearrange("(p t) n -> p t n", t=PACK))
+        nc.sync.dma_start(out=x_sb[1][:], in_=x_view[:, 1, :])
+        wx_sb = sb("wx_sb", [P, 2 * N], U8)
+        nc.sync.dma_start(out=wx_sb[:].bitcast(I32), in_=wx_words[0].bitcast(I32))
+        for quad in range(4):
+            nc.sync.dma_start(
+                out=wx_plane[32 * quad : 32 * quad + 4, :].bitcast(I32),
+                in_=wx_scales[0, 4 * quad : 4 * quad + 4, :].bitcast(I32),
+            )
+        bias = sb("bias", [P, N_TILES], F32)
+        with nc.allow_non_contiguous_dma(reason="one bias value a partition"):
+            nc.sync.dma_start(out=bias[:], in_=b.rearrange("(a p) -> p a", p=P))
+        nc.sync.dma_start(out=x_sb[2][:], in_=x_view[:, 2, :])
+        nc.sync.dma_start(out=x_sb[3][:], in_=x_view[:, 3, :])
+
+        tiers, c_back, cr_bf = {}, {}, {}
+
+        def by_unit(q, tier, pair):
+            codes, scales = pair
+            for h in range(C_WIDTHS[q] // P):
+                cols = slice(h * P, (h + 1) * P)
+                tiers[tier, c_starts[q] // P + h] = (codes[:, cols].bitcast(FP8X4), scales[:, cols])
+
+        def first_tier(q):
+            c_bf = sb("c_bf%d" % q, [P, C_WIDTHS[q] * PACK], BF16)
+            nc.scalar.copy(out=woven(c_bf[:]), in_=planes(c_raw[q][:]))
+            by_unit(q, 0, quantise("cq%d" % q, c_bf[:], C_WIDTHS[q]))
+            for h in range(C_WIDTHS[q] // P):
+                unit = c_starts[q] // P + h
+                bank = psum.tile([P, BANK], F32, name="bank%d" % unit)
+                codes, scales = tiers[0, unit]
+                for t in range(PACK):
+                    rows = slice(t * P, (t + 1) * P)
+                    nc.tensor.matmul_mx(
+                        out=bank[:, rows],
+                        lhsT=eye_codes[:, rows].bitcast(FP8X4),
+                        lhsT_scale=eye_scales[:, rows],
+                        rhs=codes,
+                        rhs_scale=scales,
+                        start=True,
+                        stop=True,
+                    )
+                c_back[q, h] = bank
+
+        def leftover(q):
+            cr_bf[q] = sb("cr_bf%d" % q, [P, C_WIDTHS[q] * PACK], BF16)
+            for h in range(C_WIDTHS[q] // P):
+                nc.vector.tensor_tensor(
+                    out=woven(cr_bf[q][:, h * BANK : (h + 1) * BANK]),
+                    in0=planes(c_raw[q][:, :, h * P : (h + 1) * P]),
+                    in1=planes(c_back[q, h][:].rearrange("p (t j) -> p t j", t=PACK)),
+                    op=SUBTRACT,
+                )
+
+        def second_tier(q):
+            by_unit(q, 1, quantise("cr%d" % q, cr_bf[q][:], C_WIDTHS[q]))
+
+        pieces = len(C_WIDTHS)
+        for q in range(pieces + 2):
+            if q < pieces:
+                first_tier(q)
+            if 0 <= q - 2:
+                second_tier(q - 2)
+            if 0 <= q - 1 < pieces:
+                leftover(q - 1)
+
+        x_starts = starts(X_WIDTHS)
+        chunks = len(X_WIDTHS)
+        y = {}
+        for q, width in enumerate(X_WIDTHS):
+            per_bank = BANK // width
+            for g in range(N_TILES // per_bank):
+                bank = psum.tile([P, BANK], F32, name="bank%d" % (UNITS - 1 - x_starts[q] // P - g))
+                y[q, g] = bank
+                first = True
+                for tier in (1, 0):
+                    for a in range(per_bank):
+                        n0 = (per_bank * g + a) * P
+                        for h in range(width // P):
+                            codes, scales = tiers[tier, x_starts[q] // P + h]
+                            nc.tensor.matmul_mx(
+                                out=bank[:, a * width + h * P : a * width + (h + 1) * P],
+                                lhsT=wx_sb[:, 2 * n0 : 2 * (n0 + P)].bitcast(FP4X4),
+                                lhsT_scale=wx_plane[:, n0 : n0 + P],
+                                rhs=codes,
+                                rhs_scale=scales,
+                                start=first,
+                                stop=False,
+                            )
+                            first = False
+
+        picked = sb("c_raw%d" % (pieces - 1), [P, PACK * J], F32)
+        xg_bf = [sb("xg_bf%d" % q, [P, w, PACK], BF16) for q, w in enumerate(X_WIDTHS)]
+
+        def chunk_planes(q):
+            j0 = x_starts[q]
+            return picked[:, PACK * j0 : PACK * (j0 + X_WIDTHS[q])].rearrange("p (t j) -> p t j", t=PACK)
+
+        def gather(t, q):
+            j0, j1 = x_starts[q], x_starts[q] + X_WIDTHS[q]
+            nc.vector.tensor_tensor(
+                out=chunk_planes(q)[:, t, :],
+                in0=x_sb[t][:].indirect(offsets[:, j0 // 16 : j1 // 16]),
+                in1=wgt_sb[:, j0:j1],
+                op=MULT,
+            )
+
+        def weave_pair(q, t0, copy):
+            copy(out=xg_bf[q][:, :, t0 : t0 + 2], in_=chunk_planes(q)[:, t0 : t0 + 2, :].rearrange("p t j -> p j t"))
+
+        for q in range(chunks):
+            gather(0, q)
+        wt_bf = sb("wt_bf", [P, N * PACK], BF16)
+        nc.scalar.copy(out=woven(wt_bf[:]), in_=planes(wt_raw[:]))
+        wt_codes, wt_scales = quantise("wt", wt_bf[:], N)
+        for q in range(chunks):
+            gather(1, q)
+            weave_pair(q, 0, nc.scalar.copy)
+        for q in range(chunks):
+            gather(2, q)
+
+        out_view = out.rearrange("(a p) j -> p a j", p=P)
+
+        def finish(q):
+            width = X_WIDTHS[q]
+            per_bank = BANK // width
+            codes, scales = quantise("xg%d" % q, xg_bf[q][:].rearrange("p j t -> p (j t)"), width)
+            for g in range(N_TILES // per_bank):
+                bank = y[q, g]
+                for a in range(per_bank):
+                    n0 = (per_bank * g + a) * P
+                    nc.tensor.matmul_mx(
+                        out=bank[:, a * width : (a + 1) * width],
+                        lhsT=wt_codes[:, n0 : n0 + P].bitcast(FP8X4),
+                        lhsT_scale=wt_scales[:, n0 : n0 + P],
+                        rhs=codes[:].bitcast(FP8X4),
+                        rhs_scale=scales[:],
+                        start=False,
+                        stop=(a == per_bank - 1),
+                    )
+                result = sb("result%d_%d" % (q, g), [P, per_bank, width], F32)
+                for a in range(per_bank):
+                    nc.scalar.activation(
+                        out=result[:, a, :],
+                        in_=bank[:, a * width : (a + 1) * width],
+                        func=GELU,
+                        bias=bias[:, per_bank * g + a : per_bank * g + a + 1],
+                    )
+                nc.sync.dma_start(
+                    out=out_view[:, per_bank * g : per_bank * (g + 1), x_starts[q] : x_starts[q] + width],
+                    in_=result[:],
+                )
+
+        for q in range(chunks):
+            gather(3, q)
+            weave_pair(q, 2, nc.scalar.copy if q in SCALAR_LATE else nc.vector.tensor_copy)
+            finish(q)

@@ -25,8 +25,10 @@ N_TILES = N // P
 BANK = 512
 UNITS = J // P
 C_WIDTHS = (128, 128, 256, 256, 256)
+C_LOADS = (128, 128, 256, 512)
 X_WIDTHS = (256, 256, 256, 128, 128)
-SCALAR_LATE = ()
+LATE_BUFS = 2
+SCALAR_LATE = (1,)
 
 
 def starts(widths):
@@ -73,8 +75,6 @@ def tile_list_gelu_kernel(tc, xT, wgt, wt, c, wx_words, wx_scales, b, offs, out)
         nc.vector.tensor_tensor_scan(out=column[:], data0=ones[:], data1=ones[:], initial=0.0, op0=MULT, op1=ADD)
         row = sb("row", [P, 32], F32)
         nc.vector.transpose(out=row[:], in_=counted[:])
-        wx_plane = sb("wx_plane", [P, N], U8)
-        nc.vector.memset(wx_plane[:].bitcast(U32), 0)
         nc.vector.tensor_scalar(
             out=eye[:].rearrange("p (j r) -> p j r", j=PACK)[:, :, 0 : PACK * P : PACK],
             in0=column[:].unsqueeze(1).to_broadcast([P, PACK, P]),
@@ -84,11 +84,19 @@ def tile_list_gelu_kernel(tc, xT, wgt, wt, c, wx_words, wx_scales, b, offs, out)
         )
         eye_codes, eye_scales = quantise("eye", eye[:, 0 : PACK * PACK * P], PACK * P)
 
+        wx_plane = sb("wx_plane", [P, N], U8)
+        nc.vector.memset(wx_plane[:].bitcast(U32), 0)
+
         c_view = c.rearrange("(p t) j -> p t j", t=PACK)
         c_starts = starts(C_WIDTHS)
-        c_raw = [sb("c_raw%d" % q, [P, PACK, w], F32) for q, w in enumerate(C_WIDTHS)]
-        for q, w in enumerate(C_WIDTHS):
-            nc.sync.dma_start(out=c_raw[q][:], in_=c_view[:, :, c_starts[q] : c_starts[q] + w])
+
+        c_raw = []
+        for i, (j0, w) in enumerate(zip(starts(C_LOADS), C_LOADS)):
+            loaded = sb("c_load%d" % i, [P, PACK, w], F32)
+            nc.sync.dma_start(out=loaded[:], in_=c_view[:, :, j0 : j0 + w])
+            c_raw.extend(
+                loaded[:, :, s - j0 : s - j0 + width] for s, width in zip(c_starts, C_WIDTHS) if j0 <= s < j0 + w
+            )
         offsets = keep.tile([P, J // 16], U16, name="offsets")
         nc.sync.dma_start(offsets[:], offs)
         wgt_sb = sb("wgt_sb", [P, J], F32)
@@ -98,7 +106,6 @@ def tile_list_gelu_kernel(tc, xT, wgt, wt, c, wx_words, wx_scales, b, offs, out)
         nc.sync.dma_start(out=x_sb[0][:], in_=x_view[:, 0, :])
         wt_raw = sb("wt_raw", [P, PACK, N], F32)
         nc.sync.dma_start(out=wt_raw[:], in_=wt.rearrange("(p t) n -> p t n", t=PACK))
-        nc.sync.dma_start(out=x_sb[1][:], in_=x_view[:, 1, :])
         wx_sb = sb("wx_sb", [P, 2 * N], U8)
         nc.sync.dma_start(out=wx_sb[:].bitcast(I32), in_=wx_words[0].bitcast(I32))
         for quad in range(4):
@@ -106,11 +113,12 @@ def tile_list_gelu_kernel(tc, xT, wgt, wt, c, wx_words, wx_scales, b, offs, out)
                 out=wx_plane[32 * quad : 32 * quad + 4, :].bitcast(I32),
                 in_=wx_scales[0, 4 * quad : 4 * quad + 4, :].bitcast(I32),
             )
+        nc.sync.dma_start(out=x_sb[1][:], in_=x_view[:, 1, :])
         bias = sb("bias", [P, N_TILES], F32)
         with nc.allow_non_contiguous_dma(reason="one bias value a partition"):
             nc.sync.dma_start(out=bias[:], in_=b.rearrange("(a p) -> p a", p=P))
-        nc.sync.dma_start(out=x_sb[2][:], in_=x_view[:, 2, :])
-        nc.sync.dma_start(out=x_sb[3][:], in_=x_view[:, 3, :])
+        for t in range(2, PACK):
+            nc.sync.dma_start(out=x_sb[t][:], in_=x_view[:, t, :])
 
         tiers, c_back, cr_bf = {}, {}, {}
 
@@ -122,7 +130,7 @@ def tile_list_gelu_kernel(tc, xT, wgt, wt, c, wx_words, wx_scales, b, offs, out)
 
         def first_tier(q):
             c_bf = sb("c_bf%d" % q, [P, C_WIDTHS[q] * PACK], BF16)
-            nc.scalar.copy(out=woven(c_bf[:]), in_=planes(c_raw[q][:]))
+            nc.scalar.copy(out=woven(c_bf[:]), in_=planes(c_raw[q]))
             by_unit(q, 0, quantise("cq%d" % q, c_bf[:], C_WIDTHS[q]))
             for h in range(C_WIDTHS[q] // P):
                 unit = c_starts[q] // P + h
@@ -142,7 +150,7 @@ def tile_list_gelu_kernel(tc, xT, wgt, wt, c, wx_words, wx_scales, b, offs, out)
                 c_back[q, h] = bank
 
         def leftover(q):
-            cr_bf[q] = sb("cr_bf%d" % q, [P, C_WIDTHS[q] * PACK], BF16)
+            cr_bf[q] = sb("c_bf%d" % (q + 1), [P, C_WIDTHS[q] * PACK], BF16)
             for h in range(C_WIDTHS[q] // P):
                 nc.vector.tensor_tensor(
                     out=woven(cr_bf[q][:, h * BANK : (h + 1) * BANK]),
@@ -169,7 +177,7 @@ def tile_list_gelu_kernel(tc, xT, wgt, wt, c, wx_words, wx_scales, b, offs, out)
         for q, width in enumerate(X_WIDTHS):
             per_bank = BANK // width
             for g in range(N_TILES // per_bank):
-                bank = psum.tile([P, BANK], F32, name="bank%d" % (UNITS - 1 - x_starts[q] // P - g))
+                bank = psum.tile([P, BANK], F32, name="bank%d" % (x_starts[q] // P + g))
                 y[q, g] = bank
                 first = True
                 for tier in (1, 0):
@@ -188,35 +196,31 @@ def tile_list_gelu_kernel(tc, xT, wgt, wt, c, wx_words, wx_scales, b, offs, out)
                             )
                             first = False
 
-        picked = sb("c_raw%d" % (pieces - 1), [P, PACK * J], F32)
         xg_bf = [sb("xg_bf%d" % q, [P, w, PACK], BF16) for q, w in enumerate(X_WIDTHS)]
+        halves = [sb("early%d" % h, [P, 2, J // 2], F32) for h in range(2)]
+        early = [halves[s // (J // 2)][:, :, s % (J // 2) : s % (J // 2) + w] for s, w in zip(x_starts, X_WIDTHS)]
+        late = {}
 
-        def chunk_planes(q):
-            j0 = x_starts[q]
-            return picked[:, PACK * j0 : PACK * (j0 + X_WIDTHS[q])].rearrange("p (t j) -> p t j", t=PACK)
-
-        def gather(t, q):
-            j0, j1 = x_starts[q], x_starts[q] + X_WIDTHS[q]
+        def gather(t, j0, j1, target):
             nc.vector.tensor_tensor(
-                out=chunk_planes(q)[:, t, :],
+                out=target,
                 in0=x_sb[t][:].indirect(offsets[:, j0 // 16 : j1 // 16]),
                 in1=wgt_sb[:, j0:j1],
                 op=MULT,
             )
 
         def weave_pair(q, t0, copy):
-            copy(out=xg_bf[q][:, :, t0 : t0 + 2], in_=chunk_planes(q)[:, t0 : t0 + 2, :].rearrange("p t j -> p j t"))
+            source = (early if t0 == 0 else late)[q]
+            copy(out=xg_bf[q][:, :, t0 : t0 + 2], in_=source.rearrange("p t j -> p j t"))
 
-        for q in range(chunks):
-            gather(0, q)
+        for h in range(2):
+            gather(0, h * J // 2, (h + 1) * J // 2, halves[h][:, 0, :])
         wt_bf = sb("wt_bf", [P, N * PACK], BF16)
         nc.scalar.copy(out=woven(wt_bf[:]), in_=planes(wt_raw[:]))
         wt_codes, wt_scales = quantise("wt", wt_bf[:], N)
         for q in range(chunks):
-            gather(1, q)
+            gather(1, x_starts[q], x_starts[q] + X_WIDTHS[q], early[q][:, 1, :])
             weave_pair(q, 0, nc.scalar.copy)
-        for q in range(chunks):
-            gather(2, q)
 
         out_view = out.rearrange("(a p) j -> p a j", p=P)
 
@@ -251,6 +255,9 @@ def tile_list_gelu_kernel(tc, xT, wgt, wt, c, wx_words, wx_scales, b, offs, out)
                 )
 
         for q in range(chunks):
-            gather(3, q)
+            pair = keep.tile([P, 2, X_WIDTHS[q]], F32, name="late", bufs=LATE_BUFS, align_bytes=64)
+            late[q] = pair[:]
+            for t in (2, 3):
+                gather(t, x_starts[q], x_starts[q] + X_WIDTHS[q], late[q][:, t - 2, :])
             weave_pair(q, 2, nc.scalar.copy if q in SCALAR_LATE else nc.vector.tensor_copy)
             finish(q)

@@ -58,6 +58,8 @@ def tile_list_gelu_kernel(tc, xT, wgt, wt, c, wx_words, wx_scales, b, offs, out)
             nc.vector.quantize_mx(out=codes[:].bitcast(FP8X4), scales=scales[:], in_=values)
             return codes, scales
 
+        wx_plane = sb("wx_plane", [P, N], U8)
+        nc.vector.memset(wx_plane[:].bitcast(U32), 0)
         ones = sb("ones", [P, P], F32)
         nc.vector.memset(ones[:], 1.0)
         first_row = sb("first_row", [P, 1], F32)
@@ -84,19 +86,30 @@ def tile_list_gelu_kernel(tc, xT, wgt, wt, c, wx_words, wx_scales, b, offs, out)
         )
         eye_codes, eye_scales = quantise("eye", eye[:, 0 : PACK * PACK * P], PACK * P)
 
-        wx_plane = sb("wx_plane", [P, N], U8)
-        nc.vector.memset(wx_plane[:].bitcast(U32), 0)
-
         c_view = c.rearrange("(p t) j -> p t j", t=PACK)
         c_starts = starts(C_WIDTHS)
 
         c_raw = []
-        for i, (j0, w) in enumerate(zip(starts(C_LOADS), C_LOADS)):
+
+        def load_c(i):
+            j0, w = starts(C_LOADS)[i], C_LOADS[i]
             loaded = sb("c_load%d" % i, [P, PACK, w], F32)
             nc.sync.dma_start(out=loaded[:], in_=c_view[:, :, j0 : j0 + w])
             c_raw.extend(
                 loaded[:, :, s - j0 : s - j0 + width] for s, width in zip(c_starts, C_WIDTHS) if j0 <= s < j0 + w
             )
+
+        load_c(0)
+        load_c(1)
+        wx_sb = sb("wx_sb", [P, 2 * N], U8)
+        nc.sync.dma_start(out=wx_sb[:].bitcast(I32), in_=wx_words[0].bitcast(I32))
+        for quad in range(4):
+            nc.sync.dma_start(
+                out=wx_plane[32 * quad : 32 * quad + 4, :].bitcast(I32),
+                in_=wx_scales[0, 4 * quad : 4 * quad + 4, :].bitcast(I32),
+            )
+        load_c(2)
+        load_c(3)
         offsets = keep.tile([P, J // 16], U16, name="offsets")
         nc.sync.dma_start(offsets[:], offs)
         wgt_sb = sb("wgt_sb", [P, J], F32)
@@ -106,19 +119,11 @@ def tile_list_gelu_kernel(tc, xT, wgt, wt, c, wx_words, wx_scales, b, offs, out)
         nc.sync.dma_start(out=x_sb[0][:], in_=x_view[:, 0, :])
         wt_raw = sb("wt_raw", [P, PACK, N], F32)
         nc.sync.dma_start(out=wt_raw[:], in_=wt.rearrange("(p t) n -> p t n", t=PACK))
-        wx_sb = sb("wx_sb", [P, 2 * N], U8)
-        nc.sync.dma_start(out=wx_sb[:].bitcast(I32), in_=wx_words[0].bitcast(I32))
-        for quad in range(4):
-            nc.sync.dma_start(
-                out=wx_plane[32 * quad : 32 * quad + 4, :].bitcast(I32),
-                in_=wx_scales[0, 4 * quad : 4 * quad + 4, :].bitcast(I32),
-            )
-        nc.sync.dma_start(out=x_sb[1][:], in_=x_view[:, 1, :])
+        for t in range(1, PACK):
+            nc.sync.dma_start(out=x_sb[t][:], in_=x_view[:, t, :])
         bias = sb("bias", [P, N_TILES], F32)
         with nc.allow_non_contiguous_dma(reason="one bias value a partition"):
             nc.sync.dma_start(out=bias[:], in_=b.rearrange("(a p) -> p a", p=P))
-        for t in range(2, PACK):
-            nc.sync.dma_start(out=x_sb[t][:], in_=x_view[:, t, :])
 
         tiers, c_back, cr_bf = {}, {}, {}
 
@@ -197,8 +202,8 @@ def tile_list_gelu_kernel(tc, xT, wgt, wt, c, wx_words, wx_scales, b, offs, out)
                             first = False
 
         xg_bf = [sb("xg_bf%d" % q, [P, w, PACK], BF16) for q, w in enumerate(X_WIDTHS)]
-        halves = [sb("early%d" % h, [P, 2, J // 2], F32) for h in range(2)]
-        early = [halves[s // (J // 2)][:, :, s % (J // 2) : s % (J // 2) + w] for s, w in zip(x_starts, X_WIDTHS)]
+        first_pair = sb("first_pair", [P, 2, J], F32)
+        early = [first_pair[:, :, s : s + w] for s, w in zip(x_starts, X_WIDTHS)]
         late = {}
 
         def gather(t, j0, j1, target):
@@ -214,7 +219,7 @@ def tile_list_gelu_kernel(tc, xT, wgt, wt, c, wx_words, wx_scales, b, offs, out)
             copy(out=xg_bf[q][:, :, t0 : t0 + 2], in_=source.rearrange("p t j -> p j t"))
 
         for h in range(2):
-            gather(0, h * J // 2, (h + 1) * J // 2, halves[h][:, 0, :])
+            gather(0, h * J // 2, (h + 1) * J // 2, first_pair[:, 0, h * J // 2 : (h + 1) * J // 2])
         wt_bf = sb("wt_bf", [P, N * PACK], BF16)
         nc.scalar.copy(out=woven(wt_bf[:]), in_=planes(wt_raw[:]))
         wt_codes, wt_scales = quantise("wt", wt_bf[:], N)

@@ -24,11 +24,11 @@ PACK = 4
 N_TILES = N // P
 BANK = 512
 UNITS = J // P
-C_WIDTHS = (128, 128, 256, 256, 256)
+C_WIDTHS = (128, 128, 128, 128, 256, 256)
 C_LOADS = (128, 128, 256, 512)
-X_WIDTHS = (256, 256, 256, 128, 128)
-LATE_BUFS = 2
-SCALAR_LATE = (1,)
+X_WIDTHS = (128, 256, 256, 256, 128)
+LEAD = 2
+SCALAR_LATE = ()
 
 
 def starts(widths):
@@ -59,7 +59,7 @@ def tile_list_gelu_kernel(tc, xT, wgt, wt, c, wx_words, wx_scales, b, offs, out)
             return codes, scales
 
         wx_plane = sb("wx_plane", [P, N], U8)
-        nc.vector.memset(wx_plane[:].bitcast(U32), 0)
+        nc.gpsimd.memset(wx_plane[:].bitcast(U32), 0)
         ones = sb("ones", [P, P], F32)
         nc.vector.memset(ones[:], 1.0)
         first_row = sb("first_row", [P, 1], F32)
@@ -68,7 +68,7 @@ def tile_list_gelu_kernel(tc, xT, wgt, wt, c, wx_words, wx_scales, b, offs, out)
         warm = sb("warm", [P, 2], F32)
         nc.scalar.activation(out=warm[:], in_=ones[:, 0:2], func=GELU)
         eye = sb("eye", [P, PACK * (PACK * P + 1)], BF16)
-        nc.vector.memset(eye[:].bitcast(U32), 0)
+        nc.gpsimd.memset(eye[:].bitcast(U32), 0)
         counted = sb("counted", [P, 32], F32)
         nc.vector.tensor_tensor_scan(
             out=counted[:], data0=ones[:, 0:32], data1=ones[:, 0:32], initial=first_row[:], op0=MULT, op1=ADD
@@ -260,9 +260,18 @@ def tile_list_gelu_kernel(tc, xT, wgt, wt, c, wx_words, wx_scales, b, offs, out)
                 )
 
         for q in range(chunks):
-            pair = keep.tile([P, 2, X_WIDTHS[q]], F32, name="late", bufs=LATE_BUFS, align_bytes=64)
-            late[q] = pair[:]
-            for t in (2, 3):
+            late[q] = sb("late%d" % q, [P, 2, X_WIDTHS[q]], F32)[:]
+
+        def late_gather(t, q):
+            if q < chunks:
                 gather(t, x_starts[q], x_starts[q] + X_WIDTHS[q], late[q][:, t - 2, :])
-            weave_pair(q, 2, nc.scalar.copy if q in SCALAR_LATE else nc.vector.tensor_copy)
-            finish(q)
+
+        for q in range(LEAD):
+            late_gather(2, q)
+        for q in range(chunks + 1):
+            late_gather(3, q)
+            if q > 0:
+                finish(q - 1)
+            late_gather(2, q + LEAD)
+            if q < chunks:
+                weave_pair(q, 2, nc.scalar.copy if q in SCALAR_LATE else nc.vector.tensor_copy)

@@ -59,7 +59,7 @@ def tile_list_gelu_kernel(tc, xT, wgt, wt, c, wx_words, wx_scales, b, offs, out)
             return codes, scales
 
         wx_plane = sb("wx_plane", [P, N], U8)
-        nc.gpsimd.memset(wx_plane[:].bitcast(U32), 0)
+        nc.vector.memset(wx_plane[:].bitcast(U32), 0)
         ones = sb("ones", [P, P], F32)
         nc.vector.memset(ones[:], 1.0)
         first_row = sb("first_row", [P, 1], F32)
@@ -68,7 +68,7 @@ def tile_list_gelu_kernel(tc, xT, wgt, wt, c, wx_words, wx_scales, b, offs, out)
         warm = sb("warm", [P, 2], F32)
         nc.scalar.activation(out=warm[:], in_=ones[:, 0:2], func=GELU)
         eye = sb("eye", [P, PACK * (PACK * P + 1)], BF16)
-        nc.gpsimd.memset(eye[:].bitcast(U32), 0)
+        nc.vector.memset(eye[:].bitcast(U32), 0)
         counted = sb("counted", [P, 32], F32)
         nc.vector.tensor_tensor_scan(
             out=counted[:], data0=ones[:, 0:32], data1=ones[:, 0:32], initial=first_row[:], op0=MULT, op1=ADD

@@ -21,14 +21,15 @@ GELU = mybir.ActivationFunctionType.Gelu_apprx_tanh
 
 P = 128
 PACK = 4
+QUAD = 32
 N_TILES = N // P
 BANK = 512
 UNITS = J // P
 C_WIDTHS = (128, 128, 128, 128, 256, 256)
-C_LOADS = (128, 128, 256, 512)
-X_WIDTHS = (128, 256, 256, 256, 128)
-LEAD = 2
-SCALAR_LATE = ()
+C_LOADS = (128, 128, 256, 256, 256)
+X_WIDTHS = (256, 256, 256, 128, 128)
+LEAD = 1
+SCALAR_LATE = (1,)
 
 
 def starts(widths):
@@ -58,32 +59,28 @@ def tile_list_gelu_kernel(tc, xT, wgt, wt, c, wx_words, wx_scales, b, offs, out)
             nc.vector.quantize_mx(out=codes[:].bitcast(FP8X4), scales=scales[:], in_=values)
             return codes, scales
 
-        wx_plane = sb("wx_plane", [P, N], U8)
-        nc.vector.memset(wx_plane[:].bitcast(U32), 0)
-        ones = sb("ones", [P, P], F32)
+        ones = sb("ones", [P, QUAD], F32)
         nc.vector.memset(ones[:], 1.0)
-        first_row = sb("first_row", [P, 1], F32)
-        for quad in range(4):
-            nc.vector.memset(first_row[32 * quad : 32 * quad + 32, :], float(32 * quad))
-        warm = sb("warm", [P, 2], F32)
-        nc.scalar.activation(out=warm[:], in_=ones[:, 0:2], func=GELU)
         eye = sb("eye", [P, PACK * (PACK * P + 1)], BF16)
         nc.vector.memset(eye[:].bitcast(U32), 0)
-        counted = sb("counted", [P, 32], F32)
-        nc.vector.tensor_tensor_scan(
-            out=counted[:], data0=ones[:, 0:32], data1=ones[:, 0:32], initial=first_row[:], op0=MULT, op1=ADD
-        )
-        column = sb("column", [P, P], F32)
+        warm = sb("warm", [P, 2], F32)
+        nc.scalar.activation(out=warm[:], in_=ones[:, 0:2], func=GELU)
+        column = sb("column", [P, QUAD], F32)
         nc.vector.tensor_tensor_scan(out=column[:], data0=ones[:], data1=ones[:], initial=0.0, op0=MULT, op1=ADD)
-        row = sb("row", [P, 32], F32)
-        nc.vector.transpose(out=row[:], in_=counted[:])
-        nc.vector.tensor_scalar(
-            out=eye[:].rearrange("p (j r) -> p j r", j=PACK)[:, :, 0 : PACK * P : PACK],
-            in0=column[:].unsqueeze(1).to_broadcast([P, PACK, P]),
-            scalar1=row[:, 0:1],
-            scalar2=None,
-            op0=IS_EQUAL,
-        )
+        row = sb("row", [P, QUAD], F32)
+        nc.vector.transpose(out=row[:], in_=column[:])
+        wx_plane = sb("wx_plane", [P, N], U8)
+        nc.vector.memset(wx_plane[:].bitcast(U32), 0)
+        diagonals = eye[:].rearrange("p (j r) -> p j r", j=PACK)
+        for quad in range(P // QUAD):
+            part = slice(QUAD * quad, QUAD * (quad + 1))
+            nc.vector.tensor_scalar(
+                out=diagonals[part, :, PACK * part.start : PACK * part.stop : PACK],
+                in0=column[part, :].unsqueeze(1).to_broadcast([QUAD, PACK, QUAD]),
+                scalar1=row[part, 0:1],
+                scalar2=None,
+                op0=IS_EQUAL,
+            )
         eye_codes, eye_scales = quantise("eye", eye[:, 0 : PACK * PACK * P], PACK * P)
 
         c_view = c.rearrange("(p t) j -> p t j", t=PACK)
@@ -99,17 +96,8 @@ def tile_list_gelu_kernel(tc, xT, wgt, wt, c, wx_words, wx_scales, b, offs, out)
                 loaded[:, :, s - j0 : s - j0 + width] for s, width in zip(c_starts, C_WIDTHS) if j0 <= s < j0 + w
             )
 
-        load_c(0)
-        load_c(1)
-        wx_sb = sb("wx_sb", [P, 2 * N], U8)
-        nc.sync.dma_start(out=wx_sb[:].bitcast(I32), in_=wx_words[0].bitcast(I32))
-        for quad in range(4):
-            nc.sync.dma_start(
-                out=wx_plane[32 * quad : 32 * quad + 4, :].bitcast(I32),
-                in_=wx_scales[0, 4 * quad : 4 * quad + 4, :].bitcast(I32),
-            )
-        load_c(2)
-        load_c(3)
+        for i in range(len(C_LOADS)):
+            load_c(i)
         offsets = keep.tile([P, J // 16], U16, name="offsets")
         nc.sync.dma_start(offsets[:], offs)
         wgt_sb = sb("wgt_sb", [P, J], F32)
@@ -117,6 +105,13 @@ def tile_list_gelu_kernel(tc, xT, wgt, wt, c, wx_words, wx_scales, b, offs, out)
         x_view = xT.rearrange("(p t) s -> p t s", t=PACK)
         x_sb = [sb("x_sb%d" % t, [P, T], F32) for t in range(PACK)]
         nc.sync.dma_start(out=x_sb[0][:], in_=x_view[:, 0, :])
+        wx_sb = sb("wx_sb", [P, 2 * N], U8)
+        nc.sync.dma_start(out=wx_sb[:].bitcast(I32), in_=wx_words[0].bitcast(I32))
+        for quad in range(4):
+            nc.sync.dma_start(
+                out=wx_plane[32 * quad : 32 * quad + 4, :].bitcast(I32),
+                in_=wx_scales[0, 4 * quad : 4 * quad + 4, :].bitcast(I32),
+            )
         wt_raw = sb("wt_raw", [P, PACK, N], F32)
         nc.sync.dma_start(out=wt_raw[:], in_=wt.rearrange("(p t) n -> p t n", t=PACK))
         for t in range(1, PACK):
@@ -222,10 +217,11 @@ def tile_list_gelu_kernel(tc, xT, wgt, wt, c, wx_words, wx_scales, b, offs, out)
             gather(0, h * J // 2, (h + 1) * J // 2, first_pair[:, 0, h * J // 2 : (h + 1) * J // 2])
         wt_bf = sb("wt_bf", [P, N * PACK], BF16)
         nc.scalar.copy(out=woven(wt_bf[:]), in_=planes(wt_raw[:]))
-        wt_codes, wt_scales = quantise("wt", wt_bf[:], N)
         for q in range(chunks):
             gather(1, x_starts[q], x_starts[q] + X_WIDTHS[q], early[q][:, 1, :])
             weave_pair(q, 0, nc.scalar.copy)
+
+        wt_codes, wt_scales = quantise("wt", wt_bf[:], N)
 
         out_view = out.rearrange("(a p) j -> p a j", p=P)
 
@@ -260,7 +256,8 @@ def tile_list_gelu_kernel(tc, xT, wgt, wt, c, wx_words, wx_scales, b, offs, out)
                 )
 
         for q in range(chunks):
-            late[q] = sb("late%d" % q, [P, 2, X_WIDTHS[q]], F32)[:]
+            held = "wt_bf" if q == 0 else "late1" if q == 1 else "xg_bf%d" % (q - 2)
+            late[q] = sb(held, [P, 2, X_WIDTHS[q]], F32)[:]
 
         def late_gather(t, q):
             if q < chunks:

@@ -29,7 +29,8 @@ C_WIDTHS = (128, 128, 128, 128, 256, 256)
 C_LOADS = (128, 128, 256, 256, 256)
 X_WIDTHS = (256, 256, 256, 128, 128)
 LEAD = 1
-SCALAR_LATE = (1,)
+SCALAR_LATE = (0, 1)
+Y_BANKS = ((6, 7), (4, 5), (0, 1), (2,), (3, 6))
 
 
 def starts(widths):
@@ -37,11 +38,11 @@ def starts(widths):
 
 
 def woven(tile):
-    return tile.rearrange("p (c i t) -> p c t i", i=2, t=PACK)
+    return tile.rearrange("p (c i t) -> p c t i", i=4, t=PACK)
 
 
 def planes(tile):
-    return tile.rearrange("p t (c i) -> p c t i", i=2)
+    return tile.rearrange("p t (c i) -> p c t i", i=4)
 
 
 def tile_list_gelu_kernel(tc, xT, wgt, wt, c, wx_words, wx_scales, b, offs, out):
@@ -100,11 +101,12 @@ def tile_list_gelu_kernel(tc, xT, wgt, wt, c, wx_words, wx_scales, b, offs, out)
             load_c(i)
         offsets = keep.tile([P, J // 16], U16, name="offsets")
         nc.sync.dma_start(offsets[:], offs)
-        wgt_sb = sb("wgt_sb", [P, J], F32)
-        nc.sync.dma_start(out=wgt_sb[:], in_=wgt)
+        wgt_sb = [sb("wgt_sb%d" % h, [P, J // 2], F32) for h in range(2)]
+        nc.sync.dma_start(out=wgt_sb[0][:], in_=wgt[:, 0 : J // 2])
         x_view = xT.rearrange("(p t) s -> p t s", t=PACK)
         x_sb = [sb("x_sb%d" % t, [P, T], F32) for t in range(PACK)]
         nc.sync.dma_start(out=x_sb[0][:], in_=x_view[:, 0, :])
+        nc.sync.dma_start(out=wgt_sb[1][:], in_=wgt[:, J // 2 : J])
         wx_sb = sb("wx_sb", [P, 2 * N], U8)
         nc.sync.dma_start(out=wx_sb[:].bitcast(I32), in_=wx_words[0].bitcast(I32))
         for quad in range(4):
@@ -113,9 +115,10 @@ def tile_list_gelu_kernel(tc, xT, wgt, wt, c, wx_words, wx_scales, b, offs, out)
                 in_=wx_scales[0, 4 * quad : 4 * quad + 4, :].bitcast(I32),
             )
         wt_raw = sb("wt_raw", [P, PACK, N], F32)
-        nc.sync.dma_start(out=wt_raw[:], in_=wt.rearrange("(p t) n -> p t n", t=PACK))
         for t in range(1, PACK):
             nc.sync.dma_start(out=x_sb[t][:], in_=x_view[:, t, :])
+            if t == 1:
+                nc.sync.dma_start(out=wt_raw[:], in_=wt.rearrange("(p t) n -> p t n", t=PACK))
         bias = sb("bias", [P, N_TILES], F32)
         with nc.allow_non_contiguous_dma(reason="one bias value a partition"):
             nc.sync.dma_start(out=bias[:], in_=b.rearrange("(a p) -> p a", p=P))
@@ -174,29 +177,37 @@ def tile_list_gelu_kernel(tc, xT, wgt, wt, c, wx_words, wx_scales, b, offs, out)
         x_starts = starts(X_WIDTHS)
         chunks = len(X_WIDTHS)
         y = {}
-        for q, width in enumerate(X_WIDTHS):
-            per_bank = BANK // width
-            for g in range(N_TILES // per_bank):
-                bank = psum.tile([P, BANK], F32, name="bank%d" % (x_starts[q] // P + g))
-                y[q, g] = bank
-                first = True
-                for tier in (1, 0):
-                    for a in range(per_bank):
-                        n0 = (per_bank * g + a) * P
-                        for h in range(width // P):
-                            codes, scales = tiers[tier, x_starts[q] // P + h]
-                            nc.tensor.matmul_mx(
-                                out=bank[:, a * width + h * P : a * width + (h + 1) * P],
-                                lhsT=wx_sb[:, 2 * n0 : 2 * (n0 + P)].bitcast(FP4X4),
-                                lhsT_scale=wx_plane[:, n0 : n0 + P],
-                                rhs=codes,
-                                rhs_scale=scales,
-                                start=first,
-                                stop=False,
-                            )
-                            first = False
 
-        xg_bf = [sb("xg_bf%d" % q, [P, w, PACK], BF16) for q, w in enumerate(X_WIDTHS)]
+        def open_sums(q, g):
+            width = X_WIDTHS[q]
+            per_bank = N_TILES // len(Y_BANKS[q])
+            bank = psum.tile([P, BANK], F32, name="bank%d" % Y_BANKS[q][g])
+            y[q, g] = bank
+            first = True
+            for tier in (1, 0):
+                for a in range(per_bank):
+                    n0 = (per_bank * g + a) * P
+                    for h in range(width // P):
+                        codes, scales = tiers[tier, x_starts[q] // P + h]
+                        nc.tensor.matmul_mx(
+                            out=bank[:, a * width + h * P : a * width + (h + 1) * P],
+                            lhsT=wx_sb[:, 2 * n0 : 2 * (n0 + P)].bitcast(FP4X4),
+                            lhsT_scale=wx_plane[:, n0 : n0 + P],
+                            rhs=codes,
+                            rhs_scale=scales,
+                            start=first,
+                            stop=False,
+                        )
+                        first = False
+
+        sums = [(q, g) for q in range(chunks) for g in range(len(Y_BANKS[q]))]
+        for q, g in sums[:-1]:
+            open_sums(q, g)
+
+        words = [2 * w for w in X_WIDTHS]
+        after_wt = sb("wt_raw", [P, sum(words)], F32)
+        region = [after_wt[:, s : s + n] for s, n in zip(starts(words), words)]
+        xg_bf = [r.bitcast(BF16).rearrange("p (j t) -> p j t", t=PACK) for r in region]
         first_pair = sb("first_pair", [P, 2, J], F32)
         early = [first_pair[:, :, s : s + w] for s, w in zip(x_starts, X_WIDTHS)]
         late = {}
@@ -205,7 +216,7 @@ def tile_list_gelu_kernel(tc, xT, wgt, wt, c, wx_words, wx_scales, b, offs, out)
             nc.vector.tensor_tensor(
                 out=target,
                 in0=x_sb[t][:].indirect(offsets[:, j0 // 16 : j1 // 16]),
-                in1=wgt_sb[:, j0:j1],
+                in1=wgt_sb[2 * j0 // J][:, j0 % (J // 2) : j0 % (J // 2) + j1 - j0],
                 op=MULT,
             )
 
@@ -213,12 +224,12 @@ def tile_list_gelu_kernel(tc, xT, wgt, wt, c, wx_words, wx_scales, b, offs, out)
             source = (early if t0 == 0 else late)[q]
             copy(out=xg_bf[q][:, :, t0 : t0 + 2], in_=source.rearrange("p t j -> p j t"))
 
-        for h in range(2):
-            gather(0, h * J // 2, (h + 1) * J // 2, first_pair[:, 0, h * J // 2 : (h + 1) * J // 2])
+        for t in range(2):
+            for h in range(2):
+                gather(t, h * J // 2, (h + 1) * J // 2, first_pair[:, t, h * J // 2 : (h + 1) * J // 2])
         wt_bf = sb("wt_bf", [P, N * PACK], BF16)
         nc.scalar.copy(out=woven(wt_bf[:]), in_=planes(wt_raw[:]))
         for q in range(chunks):
-            gather(1, x_starts[q], x_starts[q] + X_WIDTHS[q], early[q][:, 1, :])
             weave_pair(q, 0, nc.scalar.copy)
 
         wt_codes, wt_scales = quantise("wt", wt_bf[:], N)
@@ -227,8 +238,8 @@ def tile_list_gelu_kernel(tc, xT, wgt, wt, c, wx_words, wx_scales, b, offs, out)
 
         def finish(q):
             width = X_WIDTHS[q]
-            per_bank = BANK // width
-            codes, scales = quantise("xg%d" % q, xg_bf[q][:].rearrange("p j t -> p (j t)"), width)
+            per_bank = N_TILES // len(Y_BANKS[q])
+            codes, scales = quantise("xg%d" % q, region[q].bitcast(BF16), width)
             for g in range(N_TILES // per_bank):
                 bank = y[q, g]
                 for a in range(per_bank):
@@ -256,8 +267,8 @@ def tile_list_gelu_kernel(tc, xT, wgt, wt, c, wx_words, wx_scales, b, offs, out)
                 )
 
         for q in range(chunks):
-            held = "wt_bf" if q == 0 else "late1" if q == 1 else "xg_bf%d" % (q - 2)
-            late[q] = sb(held, [P, 2, X_WIDTHS[q]], F32)[:]
+            pair = sb("late%d" % q, [P, words[q]], F32)[:] if q <= LEAD else region[q - LEAD - 1][:, 0 : words[q]]
+            late[q] = pair.rearrange("p (t j) -> p t j", t=2)
 
         def late_gather(t, q):
             if q < chunks:
@@ -269,6 +280,8 @@ def tile_list_gelu_kernel(tc, xT, wgt, wt, c, wx_words, wx_scales, b, offs, out)
             late_gather(3, q)
             if q > 0:
                 finish(q - 1)
+            if q == 1:
+                open_sums(*sums[-1])
             late_gather(2, q + LEAD)
             if q < chunks:
                 weave_pair(q, 2, nc.scalar.copy if q in SCALAR_LATE else nc.vector.tensor_copy)

@@ -28,8 +28,7 @@ UNITS = J // P
 C_WIDTHS = (128, 128, 128, 128, 256, 256)
 C_LOADS = (128, 128, 256, 256, 256)
 X_WIDTHS = (256, 256, 256, 128, 128)
-LEAD = 1
-SCALAR_LATE = (0, 1)
+W_LOADS = (256, 256, 512)
 Y_BANKS = ((6, 7), (4, 5), (0, 1), (2,), (3, 6))
 
 
@@ -101,12 +100,19 @@ def tile_list_gelu_kernel(tc, xT, wgt, wt, c, wx_words, wx_scales, b, offs, out)
             load_c(i)
         offsets = keep.tile([P, J // 16], U16, name="offsets")
         nc.sync.dma_start(offsets[:], offs)
-        wgt_sb = [sb("wgt_sb%d" % h, [P, J // 2], F32) for h in range(2)]
-        nc.sync.dma_start(out=wgt_sb[0][:], in_=wgt[:, 0 : J // 2])
+        pair_b = sb("pair_b", [P, 2 * X_WIDTHS[1]], F32)
+        wgt_sb = [pair_b[:, 0 : W_LOADS[0]]] + [sb("wgt_sb%d" % i, [P, W_LOADS[i]], F32)[:] for i in (1, 2)]
+        w_starts = starts(W_LOADS)
+
+        def load_wgt(i):
+            nc.sync.dma_start(out=wgt_sb[i], in_=wgt[:, w_starts[i] : w_starts[i] + W_LOADS[i]])
+
+        load_wgt(0)
+        load_wgt(1)
         x_view = xT.rearrange("(p t) s -> p t s", t=PACK)
         x_sb = [sb("x_sb%d" % t, [P, T], F32) for t in range(PACK)]
         nc.sync.dma_start(out=x_sb[0][:], in_=x_view[:, 0, :])
-        nc.sync.dma_start(out=wgt_sb[1][:], in_=wgt[:, J // 2 : J])
+        load_wgt(2)
         wx_sb = sb("wx_sb", [P, 2 * N], U8)
         nc.sync.dma_start(out=wx_sb[:].bitcast(I32), in_=wx_words[0].bitcast(I32))
         for quad in range(4):
@@ -115,10 +121,9 @@ def tile_list_gelu_kernel(tc, xT, wgt, wt, c, wx_words, wx_scales, b, offs, out)
                 in_=wx_scales[0, 4 * quad : 4 * quad + 4, :].bitcast(I32),
             )
         wt_raw = sb("wt_raw", [P, PACK, N], F32)
+        nc.sync.dma_start(out=wt_raw[:], in_=wt.rearrange("(p t) n -> p t n", t=PACK))
         for t in range(1, PACK):
             nc.sync.dma_start(out=x_sb[t][:], in_=x_view[:, t, :])
-            if t == 1:
-                nc.sync.dma_start(out=wt_raw[:], in_=wt.rearrange("(p t) n -> p t n", t=PACK))
         bias = sb("bias", [P, N_TILES], F32)
         with nc.allow_non_contiguous_dma(reason="one bias value a partition"):
             nc.sync.dma_start(out=bias[:], in_=b.rearrange("(a p) -> p a", p=P))
@@ -213,10 +218,11 @@ def tile_list_gelu_kernel(tc, xT, wgt, wt, c, wx_words, wx_scales, b, offs, out)
         late = {}
 
         def gather(t, j0, j1, target):
+            i = [i for i, s in enumerate(w_starts) if s <= j0][-1]
             nc.vector.tensor_tensor(
                 out=target,
                 in0=x_sb[t][:].indirect(offsets[:, j0 // 16 : j1 // 16]),
-                in1=wgt_sb[2 * j0 // J][:, j0 % (J // 2) : j0 % (J // 2) + j1 - j0],
+                in1=wgt_sb[i][:, j0 - w_starts[i] : j1 - w_starts[i]],
                 op=MULT,
             )
 
@@ -225,8 +231,8 @@ def tile_list_gelu_kernel(tc, xT, wgt, wt, c, wx_words, wx_scales, b, offs, out)
             copy(out=xg_bf[q][:, :, t0 : t0 + 2], in_=source.rearrange("p t j -> p j t"))
 
         for t in range(2):
-            for h in range(2):
-                gather(t, h * J // 2, (h + 1) * J // 2, first_pair[:, t, h * J // 2 : (h + 1) * J // 2])
+            for s, w in zip(w_starts, W_LOADS):
+                gather(t, s, s + w, first_pair[:, t, s : s + w])
         wt_bf = sb("wt_bf", [P, N * PACK], BF16)
         nc.scalar.copy(out=woven(wt_bf[:]), in_=planes(wt_raw[:]))
         for q in range(chunks):
@@ -266,22 +272,30 @@ def tile_list_gelu_kernel(tc, xT, wgt, wt, c, wx_words, wx_scales, b, offs, out)
                     in_=result[:],
                 )
 
+        pair_a = sb("pair_a", [P, 2 * X_WIDTHS[0]], F32)
         for q in range(chunks):
-            pair = sb("late%d" % q, [P, words[q]], F32)[:] if q <= LEAD else region[q - LEAD - 1][:, 0 : words[q]]
-            late[q] = pair.rearrange("p (t j) -> p t j", t=2)
+            late[q] = (pair_a, pair_b)[q % 2][:, 0 : words[q]].rearrange("p (t j) -> p t j", t=2)
 
         def late_gather(t, q):
             if q < chunks:
                 gather(t, x_starts[q], x_starts[q] + X_WIDTHS[q], late[q][:, t - 2, :])
 
-        for q in range(LEAD):
+        for q in range(2):
             late_gather(2, q)
-        for q in range(chunks + 1):
             late_gather(3, q)
-            if q > 0:
-                finish(q - 1)
-            if q == 1:
-                open_sums(*sums[-1])
-            late_gather(2, q + LEAD)
-            if q < chunks:
-                weave_pair(q, 2, nc.scalar.copy if q in SCALAR_LATE else nc.vector.tensor_copy)
+            weave_pair(q, 2, nc.scalar.copy)
+        finish(0)
+        open_sums(*sums[-1])
+        late_gather(2, 2)
+        late_gather(3, 2)
+        finish(1)
+        weave_pair(2, 2, nc.vector.tensor_copy)
+        late_gather(2, 3)
+        finish(2)
+        late_gather(3, 3)
+        late_gather(2, 4)
+        weave_pair(3, 2, nc.vector.tensor_copy)
+        late_gather(3, 4)
+        finish(3)
+        weave_pair(4, 2, nc.vector.tensor_copy)
+        finish(4)

@@ -24,12 +24,12 @@ PACK = 4
 QUAD = 32
 N_TILES = N // P
 BANK = 512
-UNITS = J // P
-C_WIDTHS = (128, 128, 128, 128, 256, 256)
-C_LOADS = (128, 128, 256, 256, 256)
+PIECE = 256
+PIECES = J // PIECE
+BACK_BANKS = 4
 X_WIDTHS = (256, 256, 256, 128, 128)
-W_LOADS = (256, 256, 512)
-Y_BANKS = ((6, 7), (4, 5), (0, 1), (2,), (3, 6))
+W_LOADS = (256, 768)
+Y_BANKS = ((4, 5), (6, 7), (0, 1), (2,), (3, 4))
 
 
 def starts(widths):
@@ -83,36 +83,20 @@ def tile_list_gelu_kernel(tc, xT, wgt, wt, c, wx_words, wx_scales, b, offs, out)
             )
         eye_codes, eye_scales = quantise("eye", eye[:, 0 : PACK * PACK * P], PACK * P)
 
-        c_view = c.rearrange("(p t) j -> p t j", t=PACK)
-        c_starts = starts(C_WIDTHS)
-
-        c_raw = []
-
-        def load_c(i):
-            j0, w = starts(C_LOADS)[i], C_LOADS[i]
-            loaded = sb("c_load%d" % i, [P, PACK, w], F32)
-            nc.sync.dma_start(out=loaded[:], in_=c_view[:, :, j0 : j0 + w])
-            c_raw.extend(
-                loaded[:, :, s - j0 : s - j0 + width] for s, width in zip(c_starts, C_WIDTHS) if j0 <= s < j0 + w
-            )
-
-        for i in range(len(C_LOADS)):
-            load_c(i)
         offsets = keep.tile([P, J // 16], U16, name="offsets")
         nc.sync.dma_start(offsets[:], offs)
         pair_b = sb("pair_b", [P, 2 * X_WIDTHS[1]], F32)
-        wgt_sb = [pair_b[:, 0 : W_LOADS[0]]] + [sb("wgt_sb%d" % i, [P, W_LOADS[i]], F32)[:] for i in (1, 2)]
+        wgt_sb = [pair_b[:, 0 : W_LOADS[0]], sb("wgt_rest", [P, W_LOADS[1]], F32)[:]]
         w_starts = starts(W_LOADS)
-
-        def load_wgt(i):
-            nc.sync.dma_start(out=wgt_sb[i], in_=wgt[:, w_starts[i] : w_starts[i] + W_LOADS[i]])
-
-        load_wgt(0)
-        load_wgt(1)
         x_view = xT.rearrange("(p t) s -> p t s", t=PACK)
         x_sb = [sb("x_sb%d" % t, [P, T], F32) for t in range(PACK)]
-        nc.sync.dma_start(out=x_sb[0][:], in_=x_view[:, 0, :])
-        load_wgt(2)
+        for t in range(2):
+            nc.sync.dma_start(out=wgt_sb[t], in_=wgt[:, w_starts[t] : w_starts[t] + W_LOADS[t]])
+            nc.sync.dma_start(out=x_sb[t][:], in_=x_view[:, t, :])
+        c_view = c.rearrange("(p t) j -> p t j", t=PACK)
+        c_raw = [sb("c_raw%d" % q, [P, PACK, PIECE], F32) for q in range(PIECES)]
+        for q in range(PIECES):
+            nc.sync.dma_start(out=c_raw[q][:], in_=c_view[:, :, q * PIECE : (q + 1) * PIECE])
         wx_sb = sb("wx_sb", [P, 2 * N], U8)
         nc.sync.dma_start(out=wx_sb[:].bitcast(I32), in_=wx_words[0].bitcast(I32))
         for quad in range(4):
@@ -122,100 +106,15 @@ def tile_list_gelu_kernel(tc, xT, wgt, wt, c, wx_words, wx_scales, b, offs, out)
             )
         wt_raw = sb("wt_raw", [P, PACK, N], F32)
         nc.sync.dma_start(out=wt_raw[:], in_=wt.rearrange("(p t) n -> p t n", t=PACK))
-        for t in range(1, PACK):
+        for t in range(2, PACK):
             nc.sync.dma_start(out=x_sb[t][:], in_=x_view[:, t, :])
         bias = sb("bias", [P, N_TILES], F32)
         with nc.allow_non_contiguous_dma(reason="one bias value a partition"):
             nc.sync.dma_start(out=bias[:], in_=b.rearrange("(a p) -> p a", p=P))
 
-        tiers, c_back, cr_bf = {}, {}, {}
-
-        def by_unit(q, tier, pair):
-            codes, scales = pair
-            for h in range(C_WIDTHS[q] // P):
-                cols = slice(h * P, (h + 1) * P)
-                tiers[tier, c_starts[q] // P + h] = (codes[:, cols].bitcast(FP8X4), scales[:, cols])
-
-        def first_tier(q):
-            c_bf = sb("c_bf%d" % q, [P, C_WIDTHS[q] * PACK], BF16)
-            nc.scalar.copy(out=woven(c_bf[:]), in_=planes(c_raw[q]))
-            by_unit(q, 0, quantise("cq%d" % q, c_bf[:], C_WIDTHS[q]))
-            for h in range(C_WIDTHS[q] // P):
-                unit = c_starts[q] // P + h
-                bank = psum.tile([P, BANK], F32, name="bank%d" % unit)
-                codes, scales = tiers[0, unit]
-                for t in range(PACK):
-                    rows = slice(t * P, (t + 1) * P)
-                    nc.tensor.matmul_mx(
-                        out=bank[:, rows],
-                        lhsT=eye_codes[:, rows].bitcast(FP8X4),
-                        lhsT_scale=eye_scales[:, rows],
-                        rhs=codes,
-                        rhs_scale=scales,
-                        start=True,
-                        stop=True,
-                    )
-                c_back[q, h] = bank
-
-        def leftover(q):
-            cr_bf[q] = sb("c_bf%d" % (q + 1), [P, C_WIDTHS[q] * PACK], BF16)
-            for h in range(C_WIDTHS[q] // P):
-                nc.vector.tensor_tensor(
-                    out=woven(cr_bf[q][:, h * BANK : (h + 1) * BANK]),
-                    in0=planes(c_raw[q][:, :, h * P : (h + 1) * P]),
-                    in1=planes(c_back[q, h][:].rearrange("p (t j) -> p t j", t=PACK)),
-                    op=SUBTRACT,
-                )
-
-        def second_tier(q):
-            by_unit(q, 1, quantise("cr%d" % q, cr_bf[q][:], C_WIDTHS[q]))
-
-        pieces = len(C_WIDTHS)
-        for q in range(pieces + 2):
-            if q < pieces:
-                first_tier(q)
-            if 0 <= q - 2:
-                second_tier(q - 2)
-            if 0 <= q - 1 < pieces:
-                leftover(q - 1)
-
         x_starts = starts(X_WIDTHS)
         chunks = len(X_WIDTHS)
-        y = {}
-
-        def open_sums(q, g):
-            width = X_WIDTHS[q]
-            per_bank = N_TILES // len(Y_BANKS[q])
-            bank = psum.tile([P, BANK], F32, name="bank%d" % Y_BANKS[q][g])
-            y[q, g] = bank
-            first = True
-            for tier in (1, 0):
-                for a in range(per_bank):
-                    n0 = (per_bank * g + a) * P
-                    for h in range(width // P):
-                        codes, scales = tiers[tier, x_starts[q] // P + h]
-                        nc.tensor.matmul_mx(
-                            out=bank[:, a * width + h * P : a * width + (h + 1) * P],
-                            lhsT=wx_sb[:, 2 * n0 : 2 * (n0 + P)].bitcast(FP4X4),
-                            lhsT_scale=wx_plane[:, n0 : n0 + P],
-                            rhs=codes,
-                            rhs_scale=scales,
-                            start=first,
-                            stop=False,
-                        )
-                        first = False
-
-        sums = [(q, g) for q in range(chunks) for g in range(len(Y_BANKS[q]))]
-        for q, g in sums[:-1]:
-            open_sums(q, g)
-
-        words = [2 * w for w in X_WIDTHS]
-        after_wt = sb("wt_raw", [P, sum(words)], F32)
-        region = [after_wt[:, s : s + n] for s, n in zip(starts(words), words)]
-        xg_bf = [r.bitcast(BF16).rearrange("p (j t) -> p j t", t=PACK) for r in region]
-        first_pair = sb("first_pair", [P, 2, J], F32)
-        early = [first_pair[:, :, s : s + w] for s, w in zip(x_starts, X_WIDTHS)]
-        late = {}
+        first_pair = sb("first_pair", [P, 2 * J + PIECE], F32)
 
         def gather(t, j0, j1, target):
             i = [i for i, s in enumerate(w_starts) if s <= j0][-1]
@@ -226,16 +125,111 @@ def tile_list_gelu_kernel(tc, xT, wgt, wt, c, wx_words, wx_scales, b, offs, out)
                 op=MULT,
             )
 
+        def early_gather(t, j0, j1):
+            gather(t, j0, j1, first_pair[:, t * J + j0 : t * J + j1])
+
+        early_gather(0, 0, W_LOADS[0])
+        early_gather(0, W_LOADS[0], J)
+        early_gather(1, 0, W_LOADS[0])
+        early_gather(1, W_LOADS[0], J - PIECE)
+
+        tiers, c_back, cr_bf, y = {}, {}, {}, {}
+
+        def wx_passes(tier, q, g):
+            width = X_WIDTHS[q]
+            per_bank = N_TILES // len(Y_BANKS[q])
+            if tier == 0:
+                y[q, g] = psum.tile([P, BANK], F32, name="bank%d" % Y_BANKS[q][g])
+            codes, scales = tiers[tier, x_starts[q] // PIECE]
+            cols = slice(x_starts[q] % PIECE, x_starts[q] % PIECE + width)
+            for a in range(per_bank):
+                n0 = (per_bank * g + a) * P
+                nc.tensor.matmul_mx(
+                    out=y[q, g][:, a * width : (a + 1) * width],
+                    lhsT=wx_sb[:, 2 * n0 : 2 * (n0 + P)].bitcast(FP4X4),
+                    lhsT_scale=wx_plane[:, n0 : n0 + P],
+                    rhs=codes[:, cols].bitcast(FP8X4),
+                    rhs_scale=scales[:, cols],
+                    start=(tier == 0 and a == 0),
+                    stop=False,
+                )
+
+        def first_tier(q):
+            if q == 0:
+                c_bf = first_pair[:, 2 * J - PIECE : 2 * J + PIECE].bitcast(BF16)
+            else:
+                c_bf = sb("c_bf%d" % q, [P, PIECE * PACK], BF16)[:]
+            nc.scalar.copy(out=woven(c_bf), in_=planes(c_raw[q][:]))
+            codes, scales = tiers[0, q] = quantise("cq%d" % q, c_bf, PIECE)
+            for h in range(PIECE // P):
+                unit = q * PIECE // P + h
+                bank = psum.tile([P, BANK], F32, name="bank%d" % (unit % BACK_BANKS))
+                for t in range(PACK):
+                    rows = slice(t * P, (t + 1) * P)
+                    nc.tensor.matmul_mx(
+                        out=bank[:, rows],
+                        lhsT=eye_codes[:, rows].bitcast(FP8X4),
+                        lhsT_scale=eye_scales[:, rows],
+                        rhs=codes[:, h * P : (h + 1) * P].bitcast(FP8X4),
+                        rhs_scale=scales[:, h * P : (h + 1) * P],
+                        start=True,
+                        stop=True,
+                    )
+                c_back[q, h] = bank
+
+        def leftover(q):
+            cr_bf[q] = sb("cr_bf%d" % q, [P, PIECE * PACK], BF16)
+            for h in range(PIECE // P):
+                nc.vector.tensor_tensor(
+                    out=woven(cr_bf[q][:, h * BANK : (h + 1) * BANK]),
+                    in0=planes(c_raw[q][:, :, h * P : (h + 1) * P]),
+                    in1=planes(c_back[q, h][:].rearrange("p (t j) -> p t j", t=PACK)),
+                    op=SUBTRACT,
+                )
+
+        def second_tier(q):
+            tiers[1, q] = quantise("cr%d" % q, cr_bf[q][:], PIECE)
+
+        def open_sums(q, tier):
+            for g in range(len(Y_BANKS[q])):
+                wx_passes(tier, q, g)
+
+        first_tier(0)
+        early_gather(1, J - PIECE, J)
+        first_tier(1)
+        for q in range(PIECES):
+            leftover(q)
+            if q + 2 < PIECES:
+                first_tier(q + 2)
+            second_tier(q)
+            if q < 2:
+                open_sums(q, 0)
+                open_sums(q, 1)
+        for q in (2, 3):
+            open_sums(q, 0)
+            open_sums(q, 1)
+        wx_passes(0, 4, 0)
+        wx_passes(1, 4, 0)
+
+        words = [2 * w for w in X_WIDTHS]
+        pairs = first_pair[:, 0 : 2 * J].rearrange("p (t j) -> p t j", t=2)
+        early = [pairs[:, :, s : s + w] for s, w in zip(x_starts, X_WIDTHS)]
+        late, region = {}, {}
+
         def weave_pair(q, t0, copy):
             source = (early if t0 == 0 else late)[q]
-            copy(out=xg_bf[q][:, :, t0 : t0 + 2], in_=source.rearrange("p t j -> p j t"))
+            target = region[q].bitcast(BF16).rearrange("p (j t) -> p j t", t=PACK)
+            copy(out=target[:, :, t0 : t0 + 2], in_=source.rearrange("p t j -> p j t"))
 
-        for t in range(2):
-            for s, w in zip(w_starts, W_LOADS):
-                gather(t, s, s + w, first_pair[:, t, s : s + w])
+        after_c = sb("c_raw0", [P, words[0] + words[1]], F32)
+        region[0], region[1] = after_c[:, 0 : words[0]], after_c[:, words[0] :]
+        for q in range(2):
+            weave_pair(q, 0, nc.scalar.copy)
         wt_bf = sb("wt_bf", [P, N * PACK], BF16)
         nc.scalar.copy(out=woven(wt_bf[:]), in_=planes(wt_raw[:]))
-        for q in range(chunks):
+        after_wt = sb("wt_raw", [P, sum(words[2:])], F32)
+        for q, s in zip(range(2, chunks), starts(words[2:])):
+            region[q] = after_wt[:, s : s + words[q]]
             weave_pair(q, 0, nc.scalar.copy)
 
         wt_codes, wt_scales = quantise("wt", wt_bf[:], N)
@@ -277,15 +271,17 @@ def tile_list_gelu_kernel(tc, xT, wgt, wt, c, wx_words, wx_scales, b, offs, out)
             late[q] = (pair_a, pair_b)[q % 2][:, 0 : words[q]].rearrange("p (t j) -> p t j", t=2)
 
         def late_gather(t, q):
-            if q < chunks:
-                gather(t, x_starts[q], x_starts[q] + X_WIDTHS[q], late[q][:, t - 2, :])
+            gather(t, x_starts[q], x_starts[q] + X_WIDTHS[q], late[q][:, t - 2, :])
 
-        for q in range(2):
-            late_gather(2, q)
-            late_gather(3, q)
-            weave_pair(q, 2, nc.scalar.copy)
+        late_gather(2, 0)
+        late_gather(3, 0)
+        weave_pair(0, 2, nc.scalar.copy)
+        late_gather(3, 1)
+        late_gather(2, 1)
+        weave_pair(1, 2, nc.scalar.copy)
         finish(0)
-        open_sums(*sums[-1])
+        wx_passes(0, 4, 1)
+        wx_passes(1, 4, 1)
         late_gather(2, 2)
         late_gather(3, 2)
         finish(1)

@@ -28,8 +28,8 @@ PIECE = 256
 PIECES = J // PIECE
 BACK_BANKS = 4
 X_WIDTHS = (256, 256, 256, 128, 128)
-W_LOADS = (256, 768)
-Y_BANKS = ((4, 5), (6, 7), (0, 1), (2,), (3, 4))
+W_LOADS = (128, 384, 512)
+Y_BANKS = ((4, 5), (6, 7), (0, 1), (2, 3), (4, 5, 6, 7))
 
 
 def starts(widths):
@@ -85,14 +85,15 @@ def tile_list_gelu_kernel(tc, xT, wgt, wt, c, wx_words, wx_scales, b, offs, out)
 
         offsets = keep.tile([P, J // 16], U16, name="offsets")
         nc.sync.dma_start(offsets[:], offs)
-        pair_b = sb("pair_b", [P, 2 * X_WIDTHS[1]], F32)
-        wgt_sb = [pair_b[:, 0 : W_LOADS[0]], sb("wgt_rest", [P, W_LOADS[1]], F32)[:]]
-        w_starts = starts(W_LOADS)
+        wgt_sb = sb("wgt_sb", [P, J + PIECE], F32)
+        w_cuts = [slice(s, s + w) for s, w in zip(starts(W_LOADS), W_LOADS)]
         x_view = xT.rearrange("(p t) s -> p t s", t=PACK)
         x_sb = [sb("x_sb%d" % t, [P, T], F32) for t in range(PACK)]
-        for t in range(2):
-            nc.sync.dma_start(out=wgt_sb[t], in_=wgt[:, w_starts[t] : w_starts[t] + W_LOADS[t]])
-            nc.sync.dma_start(out=x_sb[t][:], in_=x_view[:, t, :])
+        nc.sync.dma_start(out=wgt_sb[:, w_cuts[0]], in_=wgt[:, w_cuts[0]])
+        nc.sync.dma_start(out=x_sb[0][:], in_=x_view[:, 0, :])
+        for cut in w_cuts[1:]:
+            nc.sync.dma_start(out=wgt_sb[:, cut], in_=wgt[:, cut])
+        nc.sync.dma_start(out=x_sb[1][:], in_=x_view[:, 1, :])
         c_view = c.rearrange("(p t) j -> p t j", t=PACK)
         c_raw = [sb("c_raw%d" % q, [P, PACK, PIECE], F32) for q in range(PIECES)]
         for q in range(PIECES):
@@ -117,21 +118,19 @@ def tile_list_gelu_kernel(tc, xT, wgt, wt, c, wx_words, wx_scales, b, offs, out)
         first_pair = sb("first_pair", [P, 2 * J + PIECE], F32)
 
         def gather(t, j0, j1, target):
-            i = [i for i, s in enumerate(w_starts) if s <= j0][-1]
             nc.vector.tensor_tensor(
                 out=target,
                 in0=x_sb[t][:].indirect(offsets[:, j0 // 16 : j1 // 16]),
-                in1=wgt_sb[i][:, j0 - w_starts[i] : j1 - w_starts[i]],
+                in1=wgt_sb[:, j0:j1],
                 op=MULT,
             )
 
         def early_gather(t, j0, j1):
             gather(t, j0, j1, first_pair[:, t * J + j0 : t * J + j1])
 
-        early_gather(0, 0, W_LOADS[0])
-        early_gather(0, W_LOADS[0], J)
-        early_gather(1, 0, W_LOADS[0])
-        early_gather(1, W_LOADS[0], J - PIECE)
+        for cut in w_cuts:
+            early_gather(0, cut.start, cut.stop)
+        early_gather(1, 0, J - PIECE)
 
         tiers, c_back, cr_bf, y = {}, {}, {}, {}
 
@@ -140,8 +139,12 @@ def tile_list_gelu_kernel(tc, xT, wgt, wt, c, wx_words, wx_scales, b, offs, out)
             per_bank = N_TILES // len(Y_BANKS[q])
             if tier == 0:
                 y[q, g] = psum.tile([P, BANK], F32, name="bank%d" % Y_BANKS[q][g])
-            codes, scales = tiers[tier, x_starts[q] // PIECE]
-            cols = slice(x_starts[q] % PIECE, x_starts[q] % PIECE + width)
+            if tier == 0:
+                codes, scales = tiers[0, x_starts[q] // PIECE]
+                cols = slice(x_starts[q] % PIECE, x_starts[q] % PIECE + width)
+            else:
+                codes, scales = tiers[1, q]
+                cols = slice(0, width)
             for a in range(per_bank):
                 n0 = (per_bank * g + a) * P
                 nc.tensor.matmul_mx(
@@ -160,7 +163,14 @@ def tile_list_gelu_kernel(tc, xT, wgt, wt, c, wx_words, wx_scales, b, offs, out)
             else:
                 c_bf = sb("c_bf%d" % q, [P, PIECE * PACK], BF16)[:]
             nc.scalar.copy(out=woven(c_bf), in_=planes(c_raw[q][:]))
-            codes, scales = tiers[0, q] = quantise("cq%d" % q, c_bf, PIECE)
+            codes, scales = tiers[0, q] = (sb("cq%d_codes" % q, [P, PIECE], U32), sb("cq%d_scales" % q, [P, PIECE], U8))
+            step = P if q == 0 else PIECE
+            for s in range(0, PIECE, step):
+                nc.vector.quantize_mx(
+                    out=codes[:, s : s + step].bitcast(FP8X4),
+                    scales=scales[:, s : s + step],
+                    in_=c_bf[:, PACK * s : PACK * (s + step)],
+                )
             for h in range(PIECE // P):
                 unit = q * PIECE // P + h
                 bank = psum.tile([P, BANK], F32, name="bank%d" % (unit % BACK_BANKS))
@@ -188,7 +198,7 @@ def tile_list_gelu_kernel(tc, xT, wgt, wt, c, wx_words, wx_scales, b, offs, out)
                 )
 
         def second_tier(q):
-            tiers[1, q] = quantise("cr%d" % q, cr_bf[q][:], PIECE)
+            tiers[1, q] = quantise("cr%d" % q, cr_bf[q][:, 0 : PACK * X_WIDTHS[q]], X_WIDTHS[q])
 
         def open_sums(q, tier):
             for g in range(len(Y_BANKS[q])):
@@ -208,8 +218,6 @@ def tile_list_gelu_kernel(tc, xT, wgt, wt, c, wx_words, wx_scales, b, offs, out)
         for q in (2, 3):
             open_sums(q, 0)
             open_sums(q, 1)
-        wx_passes(0, 4, 0)
-        wx_passes(1, 4, 0)
 
         words = [2 * w for w in X_WIDTHS]
         pairs = first_pair[:, 0 : 2 * J].rearrange("p (t j) -> p t j", t=2)
@@ -240,35 +248,40 @@ def tile_list_gelu_kernel(tc, xT, wgt, wt, c, wx_words, wx_scales, b, offs, out)
             width = X_WIDTHS[q]
             per_bank = N_TILES // len(Y_BANKS[q])
             codes, scales = quantise("xg%d" % q, region[q].bitcast(BF16), width)
-            for g in range(N_TILES // per_bank):
-                bank = y[q, g]
-                for a in range(per_bank):
-                    n0 = (per_bank * g + a) * P
+            for half in range(2):
+                tiles = range(2 * half, 2 * half + 2)
+                for a in tiles:
+                    g, place = divmod(a, per_bank)
                     nc.tensor.matmul_mx(
-                        out=bank[:, a * width : (a + 1) * width],
-                        lhsT=wt_codes[:, n0 : n0 + P].bitcast(FP8X4),
-                        lhsT_scale=wt_scales[:, n0 : n0 + P],
+                        out=y[q, g][:, place * width : (place + 1) * width],
+                        lhsT=wt_codes[:, a * P : (a + 1) * P].bitcast(FP8X4),
+                        lhsT_scale=wt_scales[:, a * P : (a + 1) * P],
                         rhs=codes[:].bitcast(FP8X4),
                         rhs_scale=scales[:],
                         start=False,
-                        stop=(a == per_bank - 1),
+                        stop=(place == per_bank - 1),
                     )
-                result = sb("result%d_%d" % (q, g), [P, per_bank, width], F32)
-                for a in range(per_bank):
+                result = sb("result%d_%d" % (q, half), [P, 2, width], F32)
+                for a in tiles:
+                    g, place = divmod(a, per_bank)
                     nc.scalar.activation(
-                        out=result[:, a, :],
-                        in_=bank[:, a * width : (a + 1) * width],
+                        out=result[:, a % 2, :],
+                        in_=y[q, g][:, place * width : (place + 1) * width],
                         func=GELU,
-                        bias=bias[:, per_bank * g + a : per_bank * g + a + 1],
+                        bias=bias[:, a : a + 1],
                     )
                 nc.sync.dma_start(
-                    out=out_view[:, per_bank * g : per_bank * (g + 1), x_starts[q] : x_starts[q] + width],
+                    out=out_view[:, tiles.start : tiles.stop, x_starts[q] : x_starts[q] + width],
                     in_=result[:],
                 )
 
         pair_a = sb("pair_a", [P, 2 * X_WIDTHS[0]], F32)
+        pair_views = (
+            pair_a[:].rearrange("p (t j) -> p t j", t=2),
+            wgt_sb[:].rearrange("p (s j) -> p s j", j=PIECE)[:, 0 :: J // PIECE, :],
+        )
         for q in range(chunks):
-            late[q] = (pair_a, pair_b)[q % 2][:, 0 : words[q]].rearrange("p (t j) -> p t j", t=2)
+            late[q] = pair_views[q % 2][:, :, 0 : X_WIDTHS[q]]
 
         def late_gather(t, q):
             gather(t, x_starts[q], x_starts[q] + X_WIDTHS[q], late[q][:, t - 2, :])
@@ -280,11 +293,13 @@ def tile_list_gelu_kernel(tc, xT, wgt, wt, c, wx_words, wx_scales, b, offs, out)
         late_gather(2, 1)
         weave_pair(1, 2, nc.scalar.copy)
         finish(0)
+        wx_passes(0, 4, 0)
         wx_passes(0, 4, 1)
-        wx_passes(1, 4, 1)
         late_gather(2, 2)
         late_gather(3, 2)
         finish(1)
+        wx_passes(0, 4, 2)
+        wx_passes(0, 4, 3)
         weave_pair(2, 2, nc.vector.tensor_copy)
         late_gather(2, 3)
         finish(2)
@@ -294,4 +309,9 @@ def tile_list_gelu_kernel(tc, xT, wgt, wt, c, wx_words, wx_scales, b, offs, out)
         late_gather(3, 4)
         finish(3)
         weave_pair(4, 2, nc.vector.tensor_copy)
+        last_codes = sb("x_sb3", [P, P], U32)
+        last_scales = sb("cr_last_scales", [P, P], U8)
+        nc.vector.quantize_mx(out=last_codes[:].bitcast(FP8X4), scales=last_scales[:], in_=cr_bf[PIECES - 1][:, BANK:])
+        tiers[1, 4] = (last_codes, last_scales)
+        open_sums(4, 1)
         finish(4)

@@ -28,7 +28,8 @@ PIECE = 256
 PIECES = J // PIECE
 BACK_BANKS = 4
 X_WIDTHS = (256, 256, 256, 128, 128)
-W_LOADS = (128, 384, 512)
+HEADS = 8
+W_PARTS = ((2, 4), (4, 8), (0, 2))
 Y_BANKS = ((4, 5), (6, 7), (0, 1), (2, 3), (4, 5, 6, 7))
 
 
@@ -59,41 +60,56 @@ def tile_list_gelu_kernel(tc, xT, wgt, wt, c, wx_words, wx_scales, b, offs, out)
             nc.vector.quantize_mx(out=codes[:].bitcast(FP8X4), scales=scales[:], in_=values)
             return codes, scales
 
-        ones = sb("ones", [P, QUAD], F32)
+        w_rows = sb("w_rows", [P, P], F32)
+        nc.scalar.dma_start(
+            out=w_rows[0 : P // 2, :], in_=wgt[0 : P : P // HEADS, :].rearrange("h (b j) -> h b j", j=P)
+        )
+        ones = sb("ones", [P, P], F32)
         nc.vector.memset(ones[:], 1.0)
-        eye = sb("eye", [P, PACK * (PACK * P + 1)], BF16)
-        nc.vector.memset(eye[:].bitcast(U32), 0)
         warm = sb("warm", [P, 2], F32)
         nc.scalar.activation(out=warm[:], in_=ones[:, 0:2], func=GELU)
-        column = sb("column", [P, QUAD], F32)
-        nc.vector.tensor_tensor_scan(out=column[:], data0=ones[:], data1=ones[:], initial=0.0, op0=MULT, op1=ADD)
+        base = sb("base", [P, 1], F32)
+        for quad in range(P // QUAD):
+            nc.vector.memset(base[QUAD * quad : QUAD * (quad + 1), :], float(QUAD * quad))
+
+        def count(name, width):
+            counted = sb(name, [P, width], F32)
+            nc.vector.tensor_tensor_scan(
+                out=counted[:], data0=ones[:, 0:width], data1=ones[:, 0:width], initial=0.0, op0=MULT, op1=ADD
+            )
+            return counted
+
+        short = count("short", QUAD)
+        column = count("column", P)
         row = sb("row", [P, QUAD], F32)
-        nc.vector.transpose(out=row[:], in_=column[:])
+        nc.vector.transpose(out=row[:], in_=short[:])
+        nc.vector.memset(w_rows[P // 2 :, :], 0.0)
         wx_plane = sb("wx_plane", [P, N], U8)
         nc.vector.memset(wx_plane[:].bitcast(U32), 0)
-        diagonals = eye[:].rearrange("p (j r) -> p j r", j=PACK)
-        for quad in range(P // QUAD):
-            part = slice(QUAD * quad, QUAD * (quad + 1))
+
+        def diagonal(target, places):
             nc.vector.tensor_scalar(
-                out=diagonals[part, :, PACK * part.start : PACK * part.stop : PACK],
-                in0=column[part, :].unsqueeze(1).to_broadcast([QUAD, PACK, QUAD]),
-                scalar1=row[part, 0:1],
-                scalar2=None,
-                op0=IS_EQUAL,
+                out=target, in0=places, scalar1=base[:], scalar2=row[:, 0:1], op0=SUBTRACT, op1=IS_EQUAL
             )
+
+        ident = sb("ident", [P, P], F32)
+        diagonal(ident[:], column[:])
+        eye = sb("eye", [P, PACK * (PACK * P + 1)], BF16)
+        eye_words = eye[:].bitcast(U32)
+        nc.vector.memset(eye_words[:, 0 : 2 * P], 0)
+        nc.vector.memset(eye_words[:, 2 * P :], 0)
+        diagonals = eye[:].rearrange("p (j r) -> p j r", j=PACK)
+        diagonal(diagonals[:, :, 0 : PACK * P : PACK], column[:].unsqueeze(1).to_broadcast([P, PACK, P]))
         eye_codes, eye_scales = quantise("eye", eye[:, 0 : PACK * PACK * P], PACK * P)
 
         offsets = keep.tile([P, J // 16], U16, name="offsets")
         nc.sync.dma_start(offsets[:], offs)
-        wgt_sb = sb("wgt_sb", [P, J + PIECE], F32)
-        w_cuts = [slice(s, s + w) for s, w in zip(starts(W_LOADS), W_LOADS)]
+        wgt_first = sb("wgt_first", [P, PIECE], F32)
+        nc.sync.dma_start(out=wgt_first[:], in_=wgt[:, 0:PIECE])
         x_view = xT.rearrange("(p t) s -> p t s", t=PACK)
         x_sb = [sb("x_sb%d" % t, [P, T], F32) for t in range(PACK)]
-        nc.sync.dma_start(out=wgt_sb[:, w_cuts[0]], in_=wgt[:, w_cuts[0]])
-        nc.sync.dma_start(out=x_sb[0][:], in_=x_view[:, 0, :])
-        for cut in w_cuts[1:]:
-            nc.sync.dma_start(out=wgt_sb[:, cut], in_=wgt[:, cut])
-        nc.sync.dma_start(out=x_sb[1][:], in_=x_view[:, 1, :])
+        for t in range(2):
+            nc.sync.dma_start(out=x_sb[t][:], in_=x_view[:, t, :])
         c_view = c.rearrange("(p t) j -> p t j", t=PACK)
         c_raw = [sb("c_raw%d" % q, [P, PACK, PIECE], F32) for q in range(PIECES)]
         for q in range(PIECES):
@@ -113,23 +129,53 @@ def tile_list_gelu_kernel(tc, xT, wgt, wt, c, wx_words, wx_scales, b, offs, out)
         with nc.allow_non_contiguous_dma(reason="one bias value a partition"):
             nc.sync.dma_start(out=bias[:], in_=b.rearrange("(a p) -> p a", p=P))
 
+        wgt_sb = sb("wgt_sb", [P, J + PIECE], F32)
+        turned = psum.tile([P, BANK], F32, name="bank4")
+        nc.tensor.transpose(turned[:, 0:P], w_rows[:], ident[:])
+        by_block = turned[:, 0 : P // 2].rearrange("p (h b) -> p b h", h=HEADS)
+        spread = sb("spread", [P, J], F32)
+        backs = []
+
+        def spread_part(i):
+            b0, b1 = W_PARTS[i]
+            nc.scalar.copy(
+                out=spread[:, b0 * P : b1 * P].rearrange("p (b h r) -> p b h r", h=HEADS, r=P // HEADS),
+                in_=by_block[:, b0:b1, :].unsqueeze(3).to_broadcast([P, b1 - b0, HEADS, P // HEADS]),
+            )
+            backs.append(psum.tile([P, BANK], F32, name="bank%d" % (5 + i)))
+            for blk in range(b0, b1):
+                nc.tensor.transpose(
+                    backs[i][:, (blk - b0) * P : (blk - b0 + 1) * P], spread[:, blk * P : (blk + 1) * P], ident[:]
+                )
+
+        def collect_part(i):
+            b0, b1 = W_PARTS[i]
+            nc.scalar.copy(out=wgt_sb[:, b0 * P : b1 * P], in_=backs[i][:, 0 : (b1 - b0) * P])
+
+        spread_part(0)
+        for i in range(len(W_PARTS)):
+            if i + 1 < len(W_PARTS):
+                spread_part(i + 1)
+            collect_part(i)
+
         x_starts = starts(X_WIDTHS)
         chunks = len(X_WIDTHS)
         first_pair = sb("first_pair", [P, 2 * J + PIECE], F32)
 
-        def gather(t, j0, j1, target):
+        def gather(t, j0, j1, target, weights=wgt_sb):
             nc.vector.tensor_tensor(
                 out=target,
                 in0=x_sb[t][:].indirect(offsets[:, j0 // 16 : j1 // 16]),
-                in1=wgt_sb[:, j0:j1],
+                in1=weights[:, j0:j1],
                 op=MULT,
             )
 
         def early_gather(t, j0, j1):
             gather(t, j0, j1, first_pair[:, t * J + j0 : t * J + j1])
 
-        for cut in w_cuts:
-            early_gather(0, cut.start, cut.stop)
+        gather(0, 0, PIECE, first_pair[:, 0:PIECE], wgt_first)
+        for b0, b1 in W_PARTS[:2]:
+            early_gather(0, b0 * P, b1 * P)
         early_gather(1, 0, J - PIECE)
 
         tiers, c_back, cr_bf, y = {}, {}, {}, {}

@@ -27,10 +27,10 @@ BANK = 512
 PIECE = 256
 PIECES = J // PIECE
 BACK_BANKS = 4
-X_WIDTHS = (256, 256, 256, 128, 128)
+WIDTHS = (256, 256, 256, 128, 128)
 HEADS = 8
-W_PARTS = ((2, 4), (4, 8), (0, 2))
-Y_BANKS = ((4, 5), (6, 7), (0, 1), (2, 3), (4, 5, 6, 7))
+W_PARTS = ((2, 4), (4, 8))
+Y_BANKS = ((4, 5), (6, 7), (0, 1), (4, 5), (6, 7, 2, 3))
 
 
 def starts(widths):
@@ -54,11 +54,14 @@ def tile_list_gelu_kernel(tc, xT, wgt, wt, c, wx_words, wx_scales, b, offs, out)
         def sb(name, shape, dtype):
             return keep.tile(shape, dtype, name=name, align_bytes=64)
 
-        def quantise(name, values, width):
-            codes = sb(name + "_codes", [P, width], U32)
-            scales = sb(name + "_scales", [P, width], U8)
-            nc.vector.quantize_mx(out=codes[:].bitcast(FP8X4), scales=scales[:], in_=values)
-            return codes, scales
+        def bank(number):
+            return psum.tile([P, BANK], F32, name="bank%d" % number)
+
+        def quantise(codes, scales, values):
+            nc.vector.quantize_mx(out=codes.bitcast(FP8X4), scales=scales, in_=values)
+
+        def mx_tiles(name, width):
+            return sb(name + "_codes", [P, width], U32), sb(name + "_scales", [P, width], U8)
 
         w_rows = sb("w_rows", [P, P], F32)
         nc.scalar.dma_start(
@@ -100,7 +103,35 @@ def tile_list_gelu_kernel(tc, xT, wgt, wt, c, wx_words, wx_scales, b, offs, out)
         nc.vector.memset(eye_words[:, 2 * P :], 0)
         diagonals = eye[:].rearrange("p (j r) -> p j r", j=PACK)
         diagonal(diagonals[:, :, 0 : PACK * P : PACK], column[:].unsqueeze(1).to_broadcast([P, PACK, P]))
-        eye_codes, eye_scales = quantise("eye", eye[:, 0 : PACK * PACK * P], PACK * P)
+        eye_codes, eye_scales = mx_tiles("eye", PACK * P)
+        quantise(eye_codes[:], eye_scales[:], eye[:, 0 : PACK * PACK * P])
+
+        wgt_rest = sb("wgt_rest", [P, J], F32)
+        turned = bank(4)
+        nc.tensor.transpose(turned[:, 0:P], w_rows[:], ident[:])
+        by_block = turned[:, 0 : P // 2].rearrange("p (h b) -> p b h", h=HEADS)
+        spread = sb("spread", [P, J], F32)
+        backs = []
+        for i, (b0, b1) in enumerate(W_PARTS):
+            nc.scalar.copy(
+                out=spread[:, b0 * P : b1 * P].rearrange("p (b h r) -> p b h r", h=HEADS, r=P // HEADS),
+                in_=by_block[:, b0:b1, :].unsqueeze(3).to_broadcast([P, b1 - b0, HEADS, P // HEADS]),
+            )
+            backs.append(bank(5 + i))
+            for blk in range(b0, b1):
+                nc.tensor.transpose(
+                    backs[i][:, (blk - b0) * P : (blk - b0 + 1) * P], spread[:, blk * P : (blk + 1) * P], ident[:]
+                )
+        for i, (b0, b1) in enumerate(W_PARTS):
+            nc.scalar.copy(out=wgt_rest[:, b0 * P : b1 * P], in_=backs[i][:, 0 : (b1 - b0) * P])
+
+        x_starts = starts(WIDTHS)
+        chunks = len(WIDTHS)
+        words = [2 * w for w in WIDTHS]
+        region_starts = [J + 2 * PIECE + s for s in starts(words)]
+        arena = sb("arena", [P, region_starts[-1] + words[-1]], F32)
+        region = [arena[:, s : s + w] for s, w in zip(region_starts, words)]
+        slot_starts = (J, J + PIECE, J, region_starts[1], region_starts[2])
 
         offsets = keep.tile([P, J // 16], U16, name="offsets")
         nc.sync.dma_start(offsets[:], offs)
@@ -108,12 +139,27 @@ def tile_list_gelu_kernel(tc, xT, wgt, wt, c, wx_words, wx_scales, b, offs, out)
         nc.sync.dma_start(out=wgt_first[:], in_=wgt[:, 0:PIECE])
         x_view = xT.rearrange("(p t) s -> p t s", t=PACK)
         x_sb = [sb("x_sb%d" % t, [P, T], F32) for t in range(PACK)]
-        for t in range(2):
-            nc.sync.dma_start(out=x_sb[t][:], in_=x_view[:, t, :])
         c_view = c.rearrange("(p t) j -> p t j", t=PACK)
-        c_raw = [sb("c_raw%d" % q, [P, PACK, PIECE], F32) for q in range(PIECES)]
-        for q in range(PIECES):
-            nc.sync.dma_start(out=c_raw[q][:], in_=c_view[:, :, q * PIECE : (q + 1) * PIECE])
+        c_raw = [
+            arena[:, region_starts[2] :].rearrange("p (t j) -> p t j", t=PACK)
+            if q == 1
+            else sb("c_raw%d" % q, [P, PACK, PIECE], F32)[:]
+            for q in range(PIECES)
+        ]
+
+        def load_x(t):
+            nc.sync.dma_start(out=x_sb[t][:], in_=x_view[:, t, :])
+
+        def load_c(q):
+            nc.sync.dma_start(out=c_raw[q], in_=c_view[:, :, q * PIECE : (q + 1) * PIECE])
+
+        load_x(0)
+        load_x(1)
+        load_c(0)
+        nc.sync.dma_start(out=w_rows[P // 2 : P // 2 + N_TILES, :], in_=b.rearrange("(a p) -> a p", p=P))
+        load_c(1)
+        load_c(2)
+        load_x(2)
         wx_sb = sb("wx_sb", [P, 2 * N], U8)
         nc.sync.dma_start(out=wx_sb[:].bitcast(I32), in_=wx_words[0].bitcast(I32))
         for quad in range(4):
@@ -123,46 +169,12 @@ def tile_list_gelu_kernel(tc, xT, wgt, wt, c, wx_words, wx_scales, b, offs, out)
             )
         wt_raw = sb("wt_raw", [P, PACK, N], F32)
         nc.sync.dma_start(out=wt_raw[:], in_=wt.rearrange("(p t) n -> p t n", t=PACK))
-        for t in range(2, PACK):
-            nc.sync.dma_start(out=x_sb[t][:], in_=x_view[:, t, :])
-        bias = sb("bias", [P, N_TILES], F32)
-        with nc.allow_non_contiguous_dma(reason="one bias value a partition"):
-            nc.sync.dma_start(out=bias[:], in_=b.rearrange("(a p) -> p a", p=P))
+        load_x(3)
+        load_c(3)
 
-        wgt_sb = sb("wgt_sb", [P, J + PIECE], F32)
-        turned = psum.tile([P, BANK], F32, name="bank4")
-        nc.tensor.transpose(turned[:, 0:P], w_rows[:], ident[:])
-        by_block = turned[:, 0 : P // 2].rearrange("p (h b) -> p b h", h=HEADS)
-        spread = sb("spread", [P, J], F32)
-        backs = []
-
-        def spread_part(i):
-            b0, b1 = W_PARTS[i]
-            nc.scalar.copy(
-                out=spread[:, b0 * P : b1 * P].rearrange("p (b h r) -> p b h r", h=HEADS, r=P // HEADS),
-                in_=by_block[:, b0:b1, :].unsqueeze(3).to_broadcast([P, b1 - b0, HEADS, P // HEADS]),
-            )
-            backs.append(psum.tile([P, BANK], F32, name="bank%d" % (5 + i)))
-            for blk in range(b0, b1):
-                nc.tensor.transpose(
-                    backs[i][:, (blk - b0) * P : (blk - b0 + 1) * P], spread[:, blk * P : (blk + 1) * P], ident[:]
-                )
-
-        def collect_part(i):
-            b0, b1 = W_PARTS[i]
-            nc.scalar.copy(out=wgt_sb[:, b0 * P : b1 * P], in_=backs[i][:, 0 : (b1 - b0) * P])
-
-        spread_part(0)
-        for i in range(len(W_PARTS)):
-            if i + 1 < len(W_PARTS):
-                spread_part(i + 1)
-            collect_part(i)
-
-        x_starts = starts(X_WIDTHS)
-        chunks = len(X_WIDTHS)
         first_pair = sb("first_pair", [P, 2 * J + PIECE], F32)
-
-        def gather(t, j0, j1, target, weights=wgt_sb):
+        def gather(t, j0, j1, target):
+            weights = wgt_first if j1 <= PIECE else wgt_rest
             nc.vector.tensor_tensor(
                 out=target,
                 in0=x_sb[t][:].indirect(offsets[:, j0 // 16 : j1 // 16]),
@@ -170,194 +182,194 @@ def tile_list_gelu_kernel(tc, xT, wgt, wt, c, wx_words, wx_scales, b, offs, out)
                 op=MULT,
             )
 
-        def early_gather(t, j0, j1):
-            gather(t, j0, j1, first_pair[:, t * J + j0 : t * J + j1])
+        gather(0, 0, PIECE, first_pair[:, 0:PIECE])
+        for b0, b1 in W_PARTS:
+            gather(0, b0 * P, b1 * P, first_pair[:, b0 * P : b1 * P])
+        gather(1, PIECE, J, first_pair[:, J + PIECE : 2 * J])
 
-        gather(0, 0, PIECE, first_pair[:, 0:PIECE], wgt_first)
-        for b0, b1 in W_PARTS[:2]:
-            early_gather(0, b0 * P, b1 * P)
-        early_gather(1, 0, J - PIECE)
+        tiers, c_back, c_bf, cr_bf, y = {}, {}, {}, {}, {}
+        rounded_first = sb("rounded_first", [P, PIECE], F32)
+        c_bf[0] = (first_pair[:, J : J + PIECE].bitcast(BF16), rounded_first[:].bitcast(BF16))
+        for q in range(1, PIECES):
+            whole = region[q - 1].bitcast(BF16) if q < 3 else sb("c_bf3", [P, PIECE * PACK], BF16)[:]
+            c_bf[q] = (whole[:, 0:BANK], whole[:, BANK:], whole)
+        for q in range(PIECES):
+            tiers[0, q] = mx_tiles("cq%d" % q, PIECE)
+            tiers[1, q] = mx_tiles("cr%d" % q, PIECE)
+            cr_bf[q] = sb("cr_bf%d" % q, [P, PIECE * PACK], BF16)
 
-        tiers, c_back, cr_bf, y = {}, {}, {}, {}
-
-        def wx_passes(tier, q, g):
-            width = X_WIDTHS[q]
-            per_bank = N_TILES // len(Y_BANKS[q])
-            if tier == 0:
-                y[q, g] = psum.tile([P, BANK], F32, name="bank%d" % Y_BANKS[q][g])
-            if tier == 0:
-                codes, scales = tiers[0, x_starts[q] // PIECE]
-                cols = slice(x_starts[q] % PIECE, x_starts[q] % PIECE + width)
-            else:
-                codes, scales = tiers[1, q]
-                cols = slice(0, width)
-            for a in range(per_bank):
-                n0 = (per_bank * g + a) * P
+        def come_back(q, h):
+            codes, scales = tiers[0, q]
+            c_back[q, h] = bank((2 * q + h) % BACK_BANKS)
+            for t in range(PACK):
+                rows = slice(t * P, (t + 1) * P)
                 nc.tensor.matmul_mx(
-                    out=y[q, g][:, a * width : (a + 1) * width],
-                    lhsT=wx_sb[:, 2 * n0 : 2 * (n0 + P)].bitcast(FP4X4),
-                    lhsT_scale=wx_plane[:, n0 : n0 + P],
-                    rhs=codes[:, cols].bitcast(FP8X4),
-                    rhs_scale=scales[:, cols],
-                    start=(tier == 0 and a == 0),
+                    out=c_back[q, h][:, rows],
+                    lhsT=eye_codes[:, rows].bitcast(FP8X4),
+                    lhsT_scale=eye_scales[:, rows],
+                    rhs=codes[:, h * P : (h + 1) * P].bitcast(FP8X4),
+                    rhs_scale=scales[:, h * P : (h + 1) * P],
+                    start=True,
+                    stop=True,
+                )
+
+        def first_tier_half(q, h):
+            cols = slice(h * P, (h + 1) * P)
+            nc.scalar.copy(out=woven(c_bf[q][h]), in_=planes(c_raw[q][:, :, cols]))
+            quantise(tiers[0, q][0][:, cols], tiers[0, q][1][:, cols], c_bf[q][h])
+            come_back(q, h)
+
+        def first_tier(q):
+            nc.scalar.copy(out=woven(c_bf[q][2]), in_=planes(c_raw[q]))
+            quantise(tiers[0, q][0][:], tiers[0, q][1][:], c_bf[q][2])
+            come_back(q, 0)
+            come_back(q, 1)
+
+        def leftover(q, h):
+            nc.vector.tensor_tensor(
+                out=woven(cr_bf[q][:, h * BANK : (h + 1) * BANK]),
+                in0=planes(c_raw[q][:, :, h * P : (h + 1) * P]),
+                in1=planes(c_back[q, h][:].rearrange("p (t j) -> p t j", t=PACK)),
+                op=SUBTRACT,
+            )
+
+        def second_tier(chunk):
+            q, s = divmod(x_starts[chunk], PIECE)
+            cols = slice(s, s + WIDTHS[chunk])
+            quantise(tiers[1, q][0][:, cols], tiers[1, q][1][:, cols], cr_bf[q][:, PACK * cols.start : PACK * cols.stop])
+
+        def wx_passes(tier, chunk):
+            width = WIDTHS[chunk]
+            per_bank = N_TILES // len(Y_BANKS[chunk])
+            q, s = divmod(x_starts[chunk], PIECE)
+            codes, scales = tiers[tier, q]
+            for a in range(N_TILES):
+                g, place = divmod(a, per_bank)
+                if tier == 0 and place == 0:
+                    y[chunk, g] = bank(Y_BANKS[chunk][g])
+                nc.tensor.matmul_mx(
+                    out=y[chunk, g][:, place * width : (place + 1) * width],
+                    lhsT=wx_sb[:, 2 * a * P : 2 * (a + 1) * P].bitcast(FP4X4),
+                    lhsT_scale=wx_plane[:, a * P : (a + 1) * P],
+                    rhs=codes[:, s : s + width].bitcast(FP8X4),
+                    rhs_scale=scales[:, s : s + width],
+                    start=(tier == 0 and place == 0),
                     stop=False,
                 )
 
-        def first_tier(q):
-            if q == 0:
-                c_bf = first_pair[:, 2 * J - PIECE : 2 * J + PIECE].bitcast(BF16)
-            else:
-                c_bf = sb("c_bf%d" % q, [P, PIECE * PACK], BF16)[:]
-            nc.scalar.copy(out=woven(c_bf), in_=planes(c_raw[q][:]))
-            codes, scales = tiers[0, q] = (sb("cq%d_codes" % q, [P, PIECE], U32), sb("cq%d_scales" % q, [P, PIECE], U8))
-            step = P if q == 0 else PIECE
-            for s in range(0, PIECE, step):
-                nc.vector.quantize_mx(
-                    out=codes[:, s : s + step].bitcast(FP8X4),
-                    scales=scales[:, s : s + step],
-                    in_=c_bf[:, PACK * s : PACK * (s + step)],
-                )
-            for h in range(PIECE // P):
-                unit = q * PIECE // P + h
-                bank = psum.tile([P, BANK], F32, name="bank%d" % (unit % BACK_BANKS))
-                for t in range(PACK):
-                    rows = slice(t * P, (t + 1) * P)
-                    nc.tensor.matmul_mx(
-                        out=bank[:, rows],
-                        lhsT=eye_codes[:, rows].bitcast(FP8X4),
-                        lhsT_scale=eye_scales[:, rows],
-                        rhs=codes[:, h * P : (h + 1) * P].bitcast(FP8X4),
-                        rhs_scale=scales[:, h * P : (h + 1) * P],
-                        start=True,
-                        stop=True,
-                    )
-                c_back[q, h] = bank
-
-        def leftover(q):
-            cr_bf[q] = sb("cr_bf%d" % q, [P, PIECE * PACK], BF16)
-            for h in range(PIECE // P):
-                nc.vector.tensor_tensor(
-                    out=woven(cr_bf[q][:, h * BANK : (h + 1) * BANK]),
-                    in0=planes(c_raw[q][:, :, h * P : (h + 1) * P]),
-                    in1=planes(c_back[q, h][:].rearrange("p (t j) -> p t j", t=PACK)),
-                    op=SUBTRACT,
-                )
-
-        def second_tier(q):
-            tiers[1, q] = quantise("cr%d" % q, cr_bf[q][:, 0 : PACK * X_WIDTHS[q]], X_WIDTHS[q])
-
-        def open_sums(q, tier):
-            for g in range(len(Y_BANKS[q])):
-                wx_passes(tier, q, g)
-
-        first_tier(0)
-        early_gather(1, J - PIECE, J)
-        first_tier(1)
-        for q in range(PIECES):
-            leftover(q)
-            if q + 2 < PIECES:
-                first_tier(q + 2)
+        first_tier_half(0, 0)
+        gather(1, 0, PIECE, first_pair[:, J : J + PIECE])
+        first_tier_half(0, 1)
+        for q in range(PIECES - 1):
+            for h in range(2):
+                leftover(q, h)
+                if q + 2 < PIECES:
+                    first_tier_half(q + 1, h)
+            if q + 2 == PIECES:
+                gather(2, 0, PIECE, arena[:, 0:PIECE])
             second_tier(q)
-            if q < 2:
-                open_sums(q, 0)
-                open_sums(q, 1)
-        for q in (2, 3):
-            open_sums(q, 0)
-            open_sums(q, 1)
+        gather(2, PIECE, J, arena[:, PIECE:J])
 
-        words = [2 * w for w in X_WIDTHS]
+        turned_bias = bank(7)
+        nc.tensor.transpose(turned_bias[:, 0:P], w_rows[:], ident[:])
+        bias = sb("bias", [P, N_TILES], F32)
+        nc.scalar.copy(out=bias[:], in_=turned_bias[:, P // 2 : P // 2 + N_TILES])
+
+        for chunk in range(PIECES - 1):
+            wx_passes(0, chunk)
+            wx_passes(1, chunk)
+
         pairs = first_pair[:, 0 : 2 * J].rearrange("p (t j) -> p t j", t=2)
-        early = [pairs[:, :, s : s + w] for s, w in zip(x_starts, X_WIDTHS)]
-        late, region = {}, {}
 
-        def weave_pair(q, t0, copy):
-            source = (early if t0 == 0 else late)[q]
-            target = region[q].bitcast(BF16).rearrange("p (j t) -> p j t", t=PACK)
+        def weave_pair(chunk, t0, copy):
+            s, width = x_starts[chunk], WIDTHS[chunk]
+            if t0 == 0:
+                source = pairs[:, :, s : s + width]
+            else:
+                first, second = s // width, slot_starts[chunk] // width
+                source = arena[:].rearrange("p (u j) -> p u j", j=width)[:, first : second + 1 : second - first, :]
+            target = region[chunk].bitcast(BF16).rearrange("p (j t) -> p j t", t=PACK)
             copy(out=target[:, :, t0 : t0 + 2], in_=source.rearrange("p t j -> p j t"))
 
-        after_c = sb("c_raw0", [P, words[0] + words[1]], F32)
-        region[0], region[1] = after_c[:, 0 : words[0]], after_c[:, words[0] :]
-        for q in range(2):
-            weave_pair(q, 0, nc.scalar.copy)
-        wt_bf = sb("wt_bf", [P, N * PACK], BF16)
-        nc.scalar.copy(out=woven(wt_bf[:]), in_=planes(wt_raw[:]))
-        after_wt = sb("wt_raw", [P, sum(words[2:])], F32)
-        for q, s in zip(range(2, chunks), starts(words[2:])):
-            region[q] = after_wt[:, s : s + words[q]]
-            weave_pair(q, 0, nc.scalar.copy)
+        for chunk in range(chunks):
+            weave_pair(chunk, 0, nc.scalar.copy)
 
-        wt_codes, wt_scales = quantise("wt", wt_bf[:], N)
+        wt_bf = sb("wt_bf", [P, N * PACK], BF16)
+        wt_mx = []
+
+        def quantise_wt(half, name):
+            cols = slice(half * PIECE, (half + 1) * PIECE)
+            rounded = wt_bf[:, PACK * cols.start : PACK * cols.stop]
+            wt_mx.append((sb(name, [P, PIECE], U32), sb("wt_scales%d" % half, [P, PIECE], U8)))
+            quantise(wt_mx[half][0][:], wt_mx[half][1][:], rounded)
+
+        for half in range(2):
+            cols = slice(half * PIECE, (half + 1) * PIECE)
+            nc.scalar.copy(out=woven(wt_bf[:, PACK * cols.start : PACK * cols.stop]), in_=planes(wt_raw[:, :, cols]))
+        quantise_wt(0, "wt_codes0")
 
         out_view = out.rearrange("(a p) j -> p a j", p=P)
+        picks = {}
 
-        def finish(q):
-            width = X_WIDTHS[q]
-            per_bank = N_TILES // len(Y_BANKS[q])
-            codes, scales = quantise("xg%d" % q, region[q].bitcast(BF16), width)
+        def finish(chunk):
+            width = WIDTHS[chunk]
+            per_bank = N_TILES // len(Y_BANKS[chunk])
+            codes, scales = picks[chunk] = mx_tiles("xg%d" % chunk, width)
+            quantise(codes[:], scales[:], region[chunk].bitcast(BF16))
             for half in range(2):
                 tiles = range(2 * half, 2 * half + 2)
                 for a in tiles:
                     g, place = divmod(a, per_bank)
                     nc.tensor.matmul_mx(
-                        out=y[q, g][:, place * width : (place + 1) * width],
-                        lhsT=wt_codes[:, a * P : (a + 1) * P].bitcast(FP8X4),
-                        lhsT_scale=wt_scales[:, a * P : (a + 1) * P],
+                        out=y[chunk, g][:, place * width : (place + 1) * width],
+                        lhsT=wt_mx[half][0][:, a % 2 * P : (a % 2 + 1) * P].bitcast(FP8X4),
+                        lhsT_scale=wt_mx[half][1][:, a % 2 * P : (a % 2 + 1) * P],
                         rhs=codes[:].bitcast(FP8X4),
                         rhs_scale=scales[:],
                         start=False,
                         stop=(place == per_bank - 1),
                     )
-                result = sb("result%d_%d" % (q, half), [P, 2, width], F32)
+                result = sb("result%d_%d" % (chunk, half), [P, 2, width], F32)
                 for a in tiles:
                     g, place = divmod(a, per_bank)
                     nc.scalar.activation(
                         out=result[:, a % 2, :],
-                        in_=y[q, g][:, place * width : (place + 1) * width],
+                        in_=y[chunk, g][:, place * width : (place + 1) * width],
                         func=GELU,
                         bias=bias[:, a : a + 1],
                     )
                 nc.sync.dma_start(
-                    out=out_view[:, tiles.start : tiles.stop, x_starts[q] : x_starts[q] + width],
+                    out=out_view[:, tiles.start : tiles.stop, x_starts[chunk] : x_starts[chunk] + width],
                     in_=result[:],
                 )
 
-        pair_a = sb("pair_a", [P, 2 * X_WIDTHS[0]], F32)
-        pair_views = (
-            pair_a[:].rearrange("p (t j) -> p t j", t=2),
-            wgt_sb[:].rearrange("p (s j) -> p s j", j=PIECE)[:, 0 :: J // PIECE, :],
-        )
-        for q in range(chunks):
-            late[q] = pair_views[q % 2][:, :, 0 : X_WIDTHS[q]]
+        def late_gather(chunk):
+            s, width = x_starts[chunk], WIDTHS[chunk]
+            gather(3, s, s + width, arena[:, slot_starts[chunk] : slot_starts[chunk] + width])
 
-        def late_gather(t, q):
-            gather(t, x_starts[q], x_starts[q] + X_WIDTHS[q], late[q][:, t - 2, :])
-
-        late_gather(2, 0)
-        late_gather(3, 0)
+        last = PIECES - 1
+        late_gather(0)
         weave_pair(0, 2, nc.scalar.copy)
-        late_gather(3, 1)
-        late_gather(2, 1)
-        weave_pair(1, 2, nc.scalar.copy)
+        late_gather(1)
+        quantise_wt(1, "wgt_first")
+        weave_pair(1, 2, nc.vector.tensor_copy)
         finish(0)
-        wx_passes(0, 4, 0)
-        wx_passes(0, 4, 1)
-        late_gather(2, 2)
-        late_gather(3, 2)
+        late_gather(2)
         finish(1)
-        wx_passes(0, 4, 2)
-        wx_passes(0, 4, 3)
         weave_pair(2, 2, nc.vector.tensor_copy)
-        late_gather(2, 3)
+        first_tier(last)
         finish(2)
-        late_gather(3, 3)
-        late_gather(2, 4)
+        late_gather(3)
+        wx_passes(0, 3)
+        leftover(last, 0)
         weave_pair(3, 2, nc.vector.tensor_copy)
-        late_gather(3, 4)
+        second_tier(3)
+        wx_passes(1, 3)
+        leftover(last, 1)
         finish(3)
+        wx_passes(0, 4)
+        late_gather(4)
+        second_tier(4)
+        wx_passes(1, 4)
         weave_pair(4, 2, nc.vector.tensor_copy)
-        last_codes = sb("x_sb3", [P, P], U32)
-        last_scales = sb("cr_last_scales", [P, P], U8)
-        nc.vector.quantize_mx(out=last_codes[:].bitcast(FP8X4), scales=last_scales[:], in_=cr_bf[PIECES - 1][:, BANK:])
-        tiers[1, 4] = (last_codes, last_scales)
-        open_sums(4, 1)
         finish(4)

@@ -29,7 +29,8 @@ PIECES = J // PIECE
 BACK_BANKS = 4
 WIDTHS = (256, 256, 256, 128, 128)
 HEADS = 8
-W_PARTS = ((2, 4), (4, 8))
+W_PARTS = ((2, 4), (4, 6), (6, 8))
+GROUPS = WIDTHS
 Y_BANKS = ((4, 5), (6, 7), (0, 1), (4, 5), (6, 7, 2, 3))
 
 
@@ -67,13 +68,16 @@ def tile_list_gelu_kernel(tc, xT, wgt, wt, c, wx_words, wx_scales, b, offs, out)
         nc.scalar.dma_start(
             out=w_rows[0 : P // 2, :], in_=wgt[0 : P : P // HEADS, :].rearrange("h (b j) -> h b j", j=P)
         )
+        base = sb("base", [P, 1], F32)
+        for quad in range(P // QUAD):
+            nc.gpsimd.memset(base[QUAD * quad : QUAD * (quad + 1), :], float(QUAD * quad))
+        nc.gpsimd.memset(w_rows[P // 2 :, :], 0.0)
         ones = sb("ones", [P, P], F32)
         nc.vector.memset(ones[:], 1.0)
         warm = sb("warm", [P, 2], F32)
         nc.scalar.activation(out=warm[:], in_=ones[:, 0:2], func=GELU)
-        base = sb("base", [P, 1], F32)
-        for quad in range(P // QUAD):
-            nc.vector.memset(base[QUAD * quad : QUAD * (quad + 1), :], float(QUAD * quad))
+        wx_plane = sb("wx_plane", [P, N], U8)
+        nc.vector.memset(wx_plane[:].bitcast(U32), 0)
 
         def count(name, width):
             counted = sb(name, [P, width], F32)
@@ -86,66 +90,52 @@ def tile_list_gelu_kernel(tc, xT, wgt, wt, c, wx_words, wx_scales, b, offs, out)
         column = count("column", P)
         row = sb("row", [P, QUAD], F32)
         nc.vector.transpose(out=row[:], in_=short[:])
-        nc.vector.memset(w_rows[P // 2 :, :], 0.0)
-        wx_plane = sb("wx_plane", [P, N], U8)
-        nc.vector.memset(wx_plane[:].bitcast(U32), 0)
 
         def diagonal(target, places):
             nc.vector.tensor_scalar(
                 out=target, in0=places, scalar1=base[:], scalar2=row[:, 0:1], op0=SUBTRACT, op1=IS_EQUAL
             )
 
+        eye = [sb("eye%d" % u, [P, 2 * (BANK + 1)], BF16) for u in range(2)]
         ident = sb("ident", [P, P], F32)
+        nc.vector.memset(eye[0][:, 0 : 2 * BANK].bitcast(U32), 0)
         diagonal(ident[:], column[:])
-        eye = sb("eye", [P, PACK * (PACK * P + 1)], BF16)
-        eye_words = eye[:].bitcast(U32)
-        nc.vector.memset(eye_words[:, 0 : 2 * P], 0)
-        nc.vector.memset(eye_words[:, 2 * P :], 0)
-        diagonals = eye[:].rearrange("p (j r) -> p j r", j=PACK)
-        diagonal(diagonals[:, :, 0 : PACK * P : PACK], column[:].unsqueeze(1).to_broadcast([P, PACK, P]))
+        nc.vector.memset(eye[1][:, 0 : 2 * BANK].bitcast(U32), 0)
         eye_codes, eye_scales = mx_tiles("eye", PACK * P)
-        quantise(eye_codes[:], eye_scales[:], eye[:, 0 : PACK * PACK * P])
-
-        wgt_rest = sb("wgt_rest", [P, J], F32)
-        turned = bank(4)
-        nc.tensor.transpose(turned[:, 0:P], w_rows[:], ident[:])
-        by_block = turned[:, 0 : P // 2].rearrange("p (h b) -> p b h", h=HEADS)
-        spread = sb("spread", [P, J], F32)
-        backs = []
-        for i, (b0, b1) in enumerate(W_PARTS):
-            nc.scalar.copy(
-                out=spread[:, b0 * P : b1 * P].rearrange("p (b h r) -> p b h r", h=HEADS, r=P // HEADS),
-                in_=by_block[:, b0:b1, :].unsqueeze(3).to_broadcast([P, b1 - b0, HEADS, P // HEADS]),
-            )
-            backs.append(bank(5 + i))
-            for blk in range(b0, b1):
-                nc.tensor.transpose(
-                    backs[i][:, (blk - b0) * P : (blk - b0 + 1) * P], spread[:, blk * P : (blk + 1) * P], ident[:]
-                )
-        for i, (b0, b1) in enumerate(W_PARTS):
-            nc.scalar.copy(out=wgt_rest[:, b0 * P : b1 * P], in_=backs[i][:, 0 : (b1 - b0) * P])
+        for u in range(2):
+            diagonals = eye[u][:].rearrange("p (j r) -> p j r", j=2)
+            diagonal(diagonals[:, :, 2 * u : 2 * u + BANK - 2 : PACK], column[:].unsqueeze(1).to_broadcast([P, 2, P]))
+        for u in range(2):
+            half = slice(u * PIECE, (u + 1) * PIECE)
+            quantise(eye_codes[:, half], eye_scales[:, half], eye[u][:, 0 : 2 * BANK])
 
         x_starts = starts(WIDTHS)
         chunks = len(WIDTHS)
         words = [2 * w for w in WIDTHS]
-        region_starts = [J + 2 * PIECE + s for s in starts(words)]
+        last_rounded = 5 * PIECE
+        region_starts = [last_rounded + 2 * PIECE + s for s in starts(words)]
         arena = sb("arena", [P, region_starts[-1] + words[-1]], F32)
         region = [arena[:, s : s + w] for s, w in zip(region_starts, words)]
-        slot_starts = (J, J + PIECE, J, region_starts[1], region_starts[2])
+        slots = (
+            (PIECE, 2 * PIECE),
+            (3 * PIECE, 4 * PIECE),
+            (0, 2 * PIECE),
+            (3 * PIECE, last_rounded),
+            (3 * PIECE + P, last_rounded + P),
+        )
 
         offsets = keep.tile([P, J // 16], U16, name="offsets")
         nc.sync.dma_start(offsets[:], offs)
-        wgt_first = sb("wgt_first", [P, PIECE], F32)
-        nc.sync.dma_start(out=wgt_first[:], in_=wgt[:, 0:PIECE])
         x_view = xT.rearrange("(p t) s -> p t s", t=PACK)
         x_sb = [sb("x_sb%d" % t, [P, T], F32) for t in range(PACK)]
         c_view = c.rearrange("(p t) j -> p t j", t=PACK)
-        c_raw = [
-            arena[:, region_starts[2] :].rearrange("p (t j) -> p t j", t=PACK)
-            if q == 1
-            else sb("c_raw%d" % q, [P, PACK, PIECE], F32)[:]
-            for q in range(PIECES)
-        ]
+        c_raw = {q: sb("c_raw%d" % q, [P, PACK, PIECE], F32)[:] for q in range(2, PIECES)}
+        c_raw[1] = arena[:, region_starts[2] :].rearrange("p (t j) -> p t j", t=PACK)
+
+        c_first = [sb("c_first%d" % h, [P, PACK, P], F32) for h in range(2)]
+
+        def raw_half(q, h):
+            return c_first[h][:] if q == 0 else c_raw[q][:, :, h * P : (h + 1) * P]
 
         def load_x(t):
             nc.sync.dma_start(out=x_sb[t][:], in_=x_view[:, t, :])
@@ -153,9 +143,14 @@ def tile_list_gelu_kernel(tc, xT, wgt, wt, c, wx_words, wx_scales, b, offs, out)
         def load_c(q):
             nc.sync.dma_start(out=c_raw[q], in_=c_view[:, :, q * PIECE : (q + 1) * PIECE])
 
+        turned = bank(4)
+        nc.tensor.transpose(turned[:, 0:P], w_rows[:], ident[:])
+        for h in range(2):
+            nc.sync.dma_start(out=c_first[h][:], in_=c_view[:, :, h * P : (h + 1) * P])
+        wgt_first = sb("wgt_first", [P, PIECE], F32)
+        nc.sync.dma_start(out=wgt_first[:], in_=wgt[:, 0:PIECE])
         load_x(0)
         load_x(1)
-        load_c(0)
         nc.sync.dma_start(out=w_rows[P // 2 : P // 2 + N_TILES, :], in_=b.rearrange("(a p) -> a p", p=P))
         load_c(1)
         load_c(2)
@@ -172,7 +167,95 @@ def tile_list_gelu_kernel(tc, xT, wgt, wt, c, wx_words, wx_scales, b, offs, out)
         load_x(3)
         load_c(3)
 
+        c_back, c_bf, y = {}, {}, {}
         first_pair = sb("first_pair", [P, 2 * J + PIECE], F32)
+        rounded = (
+            region[0].bitcast(BF16),
+            first_pair[:, 2 * J - PIECE : 2 * J + PIECE].bitcast(BF16),
+            region[0].bitcast(BF16),
+            arena[:, last_rounded : last_rounded + 2 * PIECE].bitcast(BF16),
+        )
+        for q in range(PIECES):
+            c_bf[q] = (rounded[q][:, 0:BANK], rounded[q][:, BANK:], rounded[q])
+        spread = sb("spread", [P, J], F32)
+        c_bf[0] = tuple(spread[:, s : s + PIECE].bitcast(BF16) for s in (0, 3 * P))
+        c_bf[2] = tuple(region[h][:, 0:PIECE].bitcast(BF16) for h in range(2))
+        first_codes, first_scales = mx_tiles("cq", J)
+        second = {}
+        cr_bf = sb("cr_bf", [P, J * PACK], BF16)
+
+        def come_back(q, h):
+            codes, scales = first_codes, first_scales
+            cols = slice(q * PIECE + h * P, q * PIECE + (h + 1) * P)
+            c_back[q, h] = bank((2 * q + h) % BACK_BANKS)
+            for t in range(PACK):
+                rows = slice(t * P, (t + 1) * P)
+                nc.tensor.matmul_mx(
+                    out=c_back[q, h][:, rows],
+                    lhsT=eye_codes[:, rows].bitcast(FP8X4),
+                    lhsT_scale=eye_scales[:, rows],
+                    rhs=codes[:, cols].bitcast(FP8X4),
+                    rhs_scale=scales[:, cols],
+                    start=True,
+                    stop=True,
+                )
+
+        def first_quantise(q, h):
+            cols = slice(q * PIECE + h * P, q * PIECE + (h + 1) * P)
+            quantise(first_codes[:, cols], first_scales[:, cols], c_bf[q][h])
+            come_back(q, h)
+
+        def first_tier_half(q, h):
+            nc.scalar.copy(out=woven(c_bf[q][h]), in_=planes(raw_half(q, h)))
+            first_quantise(q, h)
+
+        def leftover(q, h):
+            nc.vector.tensor_tensor(
+                out=woven(cr_bf[:, (2 * q + h) * BANK : (2 * q + h + 1) * BANK]),
+                in0=planes(raw_half(q, h)),
+                in1=planes(c_back[q, h][:].rearrange("p (t j) -> p t j", t=PACK)),
+                op=SUBTRACT,
+            )
+
+        g_starts = starts(GROUPS)
+
+        def second_tier(groups, codes=None):
+            s, width = g_starts[groups[0]], sum(GROUPS[g] for g in groups)
+            if codes is None:
+                codes = sb("cr%d_codes" % s, [P, width], U32)[:]
+            scales = sb("cr%d_scales" % s, [P, width], U8)
+            quantise(codes, scales[:], cr_bf[:, PACK * s : PACK * (s + width)])
+            for g in groups:
+                cols = slice(g_starts[g] - s, g_starts[g] - s + GROUPS[g])
+                second[g] = (codes[:, cols], scales[:, cols])
+
+        def sums(group, a):
+            width = GROUPS[group]
+            g, place = divmod(a, N_TILES // len(Y_BANKS[group]))
+            return y[group, g][:, place * width : (place + 1) * width]
+
+        def wx_passes(tier, group, closes=False):
+            per_bank = N_TILES // len(Y_BANKS[group])
+            cols = slice(g_starts[group], g_starts[group] + GROUPS[group])
+            codes, scales = second[group] if tier else (first_codes[:, cols], first_scales[:, cols])
+            for a in range(N_TILES):
+                opens = tier == 0 and a % per_bank == 0
+                if opens:
+                    y[group, a // per_bank] = bank(Y_BANKS[group][a // per_bank])
+                nc.tensor.matmul_mx(
+                    out=sums(group, a),
+                    lhsT=wx_sb[:, 2 * a * P : 2 * (a + 1) * P].bitcast(FP4X4),
+                    lhsT_scale=wx_plane[:, a * P : (a + 1) * P],
+                    rhs=codes.bitcast(FP8X4),
+                    rhs_scale=scales,
+                    start=opens,
+                    stop=(closes and a % per_bank == per_bank - 1),
+                )
+
+        def late_gather(t, chunk):
+            s, width, slot = x_starts[chunk], WIDTHS[chunk], slots[chunk][t - 2]
+            gather(t, s, s + width, arena[:, slot : slot + width])
+
         def gather(t, j0, j1, target):
             weights = wgt_first if j1 <= PIECE else wgt_rest
             nc.vector.tensor_tensor(
@@ -182,102 +265,68 @@ def tile_list_gelu_kernel(tc, xT, wgt, wt, c, wx_words, wx_scales, b, offs, out)
                 op=MULT,
             )
 
+        wgt_rest = sb("wgt_rest", [P, J], F32)
+        by_block = turned[:, 0 : P // 2].rearrange("p (h b) -> p b h", h=HEADS)
+        backs = []
+
+        def spread_blocks(b0, b1):
+            nc.scalar.copy(
+                out=spread[:, b0 * P : b1 * P].rearrange("p (b h r) -> p b h r", h=HEADS, r=P // HEADS),
+                in_=by_block[:, b0:b1, :].unsqueeze(3).to_broadcast([P, b1 - b0, HEADS, P // HEADS]),
+            )
+
+        def turn_part(i):
+            b0, b1 = W_PARTS[i]
+            backs.append(bank(5 + i))
+            for blk in range(b0, b1):
+                nc.tensor.transpose(
+                    backs[i][:, (blk - b0) * P : (blk - b0 + 1) * P], spread[:, blk * P : (blk + 1) * P], ident[:]
+                )
+
+        def collect_part(i):
+            b0, b1 = W_PARTS[i]
+            nc.scalar.copy(out=wgt_rest[:, b0 * P : b1 * P], in_=backs[i][:, 0 : (b1 - b0) * P])
+
+        first_tier_half(0, 0)
+        first_tier_half(0, 1)
+        spread_blocks(2, 4)
+        spread_blocks(4, 8)
+        for i in range(len(W_PARTS)):
+            turn_part(i)
+        for i in range(len(W_PARTS)):
+            collect_part(i)
+        leftover(0, 0)
+        leftover(0, 1)
+
         gather(0, 0, PIECE, first_pair[:, 0:PIECE])
         for b0, b1 in W_PARTS:
             gather(0, b0 * P, b1 * P, first_pair[:, b0 * P : b1 * P])
-        gather(1, PIECE, J, first_pair[:, J + PIECE : 2 * J])
-
-        tiers, c_back, c_bf, cr_bf, y = {}, {}, {}, {}, {}
-        rounded_first = sb("rounded_first", [P, PIECE], F32)
-        c_bf[0] = (first_pair[:, J : J + PIECE].bitcast(BF16), rounded_first[:].bitcast(BF16))
-        for q in range(1, PIECES):
-            whole = region[q - 1].bitcast(BF16) if q < 3 else sb("c_bf3", [P, PIECE * PACK], BF16)[:]
-            c_bf[q] = (whole[:, 0:BANK], whole[:, BANK:], whole)
-        for q in range(PIECES):
-            tiers[0, q] = mx_tiles("cq%d" % q, PIECE)
-            tiers[1, q] = mx_tiles("cr%d" % q, PIECE)
-            cr_bf[q] = sb("cr_bf%d" % q, [P, PIECE * PACK], BF16)
-
-        def come_back(q, h):
-            codes, scales = tiers[0, q]
-            c_back[q, h] = bank((2 * q + h) % BACK_BANKS)
-            for t in range(PACK):
-                rows = slice(t * P, (t + 1) * P)
-                nc.tensor.matmul_mx(
-                    out=c_back[q, h][:, rows],
-                    lhsT=eye_codes[:, rows].bitcast(FP8X4),
-                    lhsT_scale=eye_scales[:, rows],
-                    rhs=codes[:, h * P : (h + 1) * P].bitcast(FP8X4),
-                    rhs_scale=scales[:, h * P : (h + 1) * P],
-                    start=True,
-                    stop=True,
-                )
-
-        def first_tier_half(q, h):
-            cols = slice(h * P, (h + 1) * P)
-            nc.scalar.copy(out=woven(c_bf[q][h]), in_=planes(c_raw[q][:, :, cols]))
-            quantise(tiers[0, q][0][:, cols], tiers[0, q][1][:, cols], c_bf[q][h])
-            come_back(q, h)
-
-        def first_tier(q):
-            nc.scalar.copy(out=woven(c_bf[q][2]), in_=planes(c_raw[q]))
-            quantise(tiers[0, q][0][:], tiers[0, q][1][:], c_bf[q][2])
-            come_back(q, 0)
-            come_back(q, 1)
-
-        def leftover(q, h):
-            nc.vector.tensor_tensor(
-                out=woven(cr_bf[q][:, h * BANK : (h + 1) * BANK]),
-                in0=planes(c_raw[q][:, :, h * P : (h + 1) * P]),
-                in1=planes(c_back[q, h][:].rearrange("p (t j) -> p t j", t=PACK)),
-                op=SUBTRACT,
-            )
-
-        def second_tier(chunk):
-            q, s = divmod(x_starts[chunk], PIECE)
-            cols = slice(s, s + WIDTHS[chunk])
-            quantise(tiers[1, q][0][:, cols], tiers[1, q][1][:, cols], cr_bf[q][:, PACK * cols.start : PACK * cols.stop])
-
-        def wx_passes(tier, chunk):
-            width = WIDTHS[chunk]
-            per_bank = N_TILES // len(Y_BANKS[chunk])
-            q, s = divmod(x_starts[chunk], PIECE)
-            codes, scales = tiers[tier, q]
-            for a in range(N_TILES):
-                g, place = divmod(a, per_bank)
-                if tier == 0 and place == 0:
-                    y[chunk, g] = bank(Y_BANKS[chunk][g])
-                nc.tensor.matmul_mx(
-                    out=y[chunk, g][:, place * width : (place + 1) * width],
-                    lhsT=wx_sb[:, 2 * a * P : 2 * (a + 1) * P].bitcast(FP4X4),
-                    lhsT_scale=wx_plane[:, a * P : (a + 1) * P],
-                    rhs=codes[:, s : s + width].bitcast(FP8X4),
-                    rhs_scale=scales[:, s : s + width],
-                    start=(tier == 0 and place == 0),
-                    stop=False,
-                )
-
-        first_tier_half(0, 0)
         gather(1, 0, PIECE, first_pair[:, J : J + PIECE])
-        first_tier_half(0, 1)
-        for q in range(PIECES - 1):
-            for h in range(2):
-                leftover(q, h)
-                if q + 2 < PIECES:
-                    first_tier_half(q + 1, h)
-            if q + 2 == PIECES:
-                gather(2, 0, PIECE, arena[:, 0:PIECE])
-            second_tier(q)
-        gather(2, PIECE, J, arena[:, PIECE:J])
+        gather(1, PIECE, J - PIECE, first_pair[:, J + PIECE : 2 * J - PIECE])
+        nc.scalar.copy(out=woven(c_bf[1][2]), in_=planes(c_raw[1]))
+        first_quantise(1, 0)
+        first_quantise(1, 1)
+        gather(1, J - PIECE, J, first_pair[:, 2 * J - PIECE : 2 * J])
+        first_tier_half(2, 0)
+        leftover(1, 0)
+        first_tier_half(2, 1)
+        leftover(1, 1)
+        leftover(2, 0)
+        second_tier((0, 1))
+        leftover(2, 1)
+        late_gather(2, 0)
+        late_gather(2, 1)
+        late_gather(2, 2)
 
         turned_bias = bank(7)
         nc.tensor.transpose(turned_bias[:, 0:P], w_rows[:], ident[:])
         bias = sb("bias", [P, N_TILES], F32)
         nc.scalar.copy(out=bias[:], in_=turned_bias[:, P // 2 : P // 2 + N_TILES])
 
-        for chunk in range(PIECES - 1):
-            wx_passes(0, chunk)
-            wx_passes(1, chunk)
+        for group in range(2):
+            wx_passes(0, group)
+            wx_passes(1, group)
+        wx_passes(0, 2)
 
         pairs = first_pair[:, 0 : 2 * J].rearrange("p (t j) -> p t j", t=2)
 
@@ -286,7 +335,7 @@ def tile_list_gelu_kernel(tc, xT, wgt, wt, c, wx_words, wx_scales, b, offs, out)
             if t0 == 0:
                 source = pairs[:, :, s : s + width]
             else:
-                first, second = s // width, slot_starts[chunk] // width
+                first, second = (slot // width for slot in slots[chunk])
                 source = arena[:].rearrange("p (u j) -> p u j", j=width)[:, first : second + 1 : second - first, :]
             target = region[chunk].bitcast(BF16).rearrange("p (j t) -> p j t", t=PACK)
             copy(out=target[:, :, t0 : t0 + 2], in_=source.rearrange("p t j -> p j t"))
@@ -295,81 +344,77 @@ def tile_list_gelu_kernel(tc, xT, wgt, wt, c, wx_words, wx_scales, b, offs, out)
             weave_pair(chunk, 0, nc.scalar.copy)
 
         wt_bf = sb("wt_bf", [P, N * PACK], BF16)
-        wt_mx = []
-
-        def quantise_wt(half, name):
-            cols = slice(half * PIECE, (half + 1) * PIECE)
-            rounded = wt_bf[:, PACK * cols.start : PACK * cols.stop]
-            wt_mx.append((sb(name, [P, PIECE], U32), sb("wt_scales%d" % half, [P, PIECE], U8)))
-            quantise(wt_mx[half][0][:], wt_mx[half][1][:], rounded)
-
-        for half in range(2):
-            cols = slice(half * PIECE, (half + 1) * PIECE)
-            nc.scalar.copy(out=woven(wt_bf[:, PACK * cols.start : PACK * cols.stop]), in_=planes(wt_raw[:, :, cols]))
-        quantise_wt(0, "wt_codes0")
+        nc.scalar.copy(out=woven(wt_bf[:]), in_=planes(wt_raw[:]))
 
         out_view = out.rearrange("(a p) j -> p a j", p=P)
         picks = {}
 
-        def finish(chunk):
-            width = WIDTHS[chunk]
-            per_bank = N_TILES // len(Y_BANKS[chunk])
-            codes, scales = picks[chunk] = mx_tiles("xg%d" % chunk, width)
-            quantise(codes[:], scales[:], region[chunk].bitcast(BF16))
-            for half in range(2):
-                tiles = range(2 * half, 2 * half + 2)
-                for a in tiles:
-                    g, place = divmod(a, per_bank)
-                    nc.tensor.matmul_mx(
-                        out=y[chunk, g][:, place * width : (place + 1) * width],
-                        lhsT=wt_mx[half][0][:, a % 2 * P : (a % 2 + 1) * P].bitcast(FP8X4),
-                        lhsT_scale=wt_mx[half][1][:, a % 2 * P : (a % 2 + 1) * P],
-                        rhs=codes[:].bitcast(FP8X4),
-                        rhs_scale=scales[:],
-                        start=False,
-                        stop=(place == per_bank - 1),
-                    )
-                result = sb("result%d_%d" % (chunk, half), [P, 2, width], F32)
-                for a in tiles:
-                    g, place = divmod(a, per_bank)
-                    nc.scalar.activation(
-                        out=result[:, a % 2, :],
-                        in_=y[chunk, g][:, place * width : (place + 1) * width],
-                        func=GELU,
-                        bias=bias[:, a : a + 1],
-                    )
-                nc.sync.dma_start(
-                    out=out_view[:, tiles.start : tiles.stop, x_starts[chunk] : x_starts[chunk] + width],
-                    in_=result[:],
+        def project(group, closes=True):
+            width = GROUPS[group]
+            per_bank = N_TILES // len(Y_BANKS[group])
+            codes, scales = picks[group] = mx_tiles("xg%d" % group, width)
+            s = region_starts[0] + 2 * g_starts[group]
+            quantise(codes[:], scales[:], arena[:, s : s + 2 * width].bitcast(BF16))
+            for a in range(N_TILES):
+                nc.tensor.matmul_mx(
+                    out=sums(group, a),
+                    lhsT=wt_codes[:, a * P : (a + 1) * P].bitcast(FP8X4),
+                    lhsT_scale=wt_scales[:, a * P : (a + 1) * P],
+                    rhs=codes[:].bitcast(FP8X4),
+                    rhs_scale=scales[:],
+                    start=False,
+                    stop=(closes and a % per_bank == per_bank - 1),
                 )
 
-        def late_gather(chunk):
-            s, width = x_starts[chunk], WIDTHS[chunk]
-            gather(3, s, s + width, arena[:, slot_starts[chunk] : slot_starts[chunk] + width])
+        def finish(group):
+            width = GROUPS[group]
+            per_store = 1 if width == BANK else 2
+            for a0 in range(0, N_TILES, per_store):
+                result = sb("result%d_%d" % (group, a0), [P, per_store, width], F32)
+                for a in range(a0, a0 + per_store):
+                    nc.scalar.activation(
+                        out=result[:, a - a0, :], in_=sums(group, a), func=GELU, bias=bias[:, a : a + 1]
+                    )
+                nc.sync.dma_start(
+                    out=out_view[:, a0 : a0 + per_store, g_starts[group] : g_starts[group] + width], in_=result[:]
+                )
 
         last = PIECES - 1
-        late_gather(0)
+        late_gather(3, 0)
         weave_pair(0, 2, nc.scalar.copy)
-        late_gather(1)
-        quantise_wt(1, "wgt_first")
-        weave_pair(1, 2, nc.vector.tensor_copy)
+        late_gather(3, 1)
+        weave_pair(1, 2, nc.scalar.copy)
+        held = sb("wgt_first", [P, N + PIECE], U32)
+        wt_codes, wt_scales = held[:, 0:N], sb("wt_scales", [P, N], U8)
+        quantise(wt_codes, wt_scales[:], wt_bf[:])
+        project(0)
+        late_gather(3, 2)
+        project(1)
+        nc.scalar.copy(out=woven(c_bf[last][2]), in_=planes(c_raw[last]))
         finish(0)
-        late_gather(2)
         finish(1)
         weave_pair(2, 2, nc.vector.tensor_copy)
-        first_tier(last)
+        second_tier((2,), held[:, N:])
+        wx_passes(1, 2)
+        first_quantise(last, 0)
+        first_quantise(last, 1)
+        late_gather(2, 3)
+        late_gather(2, 4)
+        project(2)
         finish(2)
-        late_gather(3)
+        late_gather(3, 3)
+        late_gather(3, 4)
         wx_passes(0, 3)
         leftover(last, 0)
         weave_pair(3, 2, nc.vector.tensor_copy)
-        second_tier(3)
+        second_tier((3,))
         wx_passes(1, 3)
-        leftover(last, 1)
-        finish(3)
-        wx_passes(0, 4)
-        late_gather(4)
-        second_tier(4)
-        wx_passes(1, 4)
         weave_pair(4, 2, nc.vector.tensor_copy)
+        project(3)
+        finish(3)
+        leftover(last, 1)
+        wx_passes(0, 4)
+        project(4, closes=False)
+        second_tier((4,))
+        wx_passes(1, 4, closes=True)
         finish(4)

@@ -31,6 +31,7 @@ WIDTHS = (256, 256, 256, 128, 128)
 HEADS = 8
 W_PARTS = ((2, 4), (4, 6), (6, 8))
 GROUPS = WIDTHS
+STORES = ((0, 1), (1, 2), (2, 2), (3, 2), (4, 2))
 Y_BANKS = ((4, 5), (6, 7), (0, 1), (4, 5), (6, 7, 2, 3))
 
 
@@ -366,18 +367,23 @@ def tile_list_gelu_kernel(tc, xT, wgt, wt, c, wx_words, wx_scales, b, offs, out)
                     stop=(closes and a % per_bank == per_bank - 1),
                 )
 
+        results = {}
+
         def finish(group):
-            width = GROUPS[group]
-            per_store = 1 if width == BANK else 2
+            first, per_store = STORES[group]
+            j0 = g_starts[first]
+            s, width = g_starts[group] - j0, GROUPS[group]
+            span = sum(w for g, w in enumerate(GROUPS) if STORES[g][0] == first)
             for a0 in range(0, N_TILES, per_store):
-                result = sb("result%d_%d" % (group, a0), [P, per_store, width], F32)
+                if group == first:
+                    results[first, a0] = sb("result%d_%d" % (group, a0), [P, per_store, span], F32)
+                result = results[first, a0]
                 for a in range(a0, a0 + per_store):
                     nc.scalar.activation(
-                        out=result[:, a - a0, :], in_=sums(group, a), func=GELU, bias=bias[:, a : a + 1]
+                        out=result[:, a - a0, s : s + width], in_=sums(group, a), func=GELU, bias=bias[:, a : a + 1]
                     )
-                nc.sync.dma_start(
-                    out=out_view[:, a0 : a0 + per_store, g_starts[group] : g_starts[group] + width], in_=result[:]
-                )
+                if s + width == span:
+                    nc.sync.dma_start(out=out_view[:, a0 : a0 + per_store, j0 : j0 + span], in_=result[:])
 
         last = PIECES - 1
         late_gather(3, 0)

@@ -25,13 +25,11 @@ QUAD = 32
 N_TILES = N // P
 BANK = 512
 PIECE = 256
-PIECES = J // PIECE
+C_LOADS = (1, 2, 3, 2)
 BACK_BANKS = 4
 WIDTHS = (256, 256, 256, 128, 128)
 HEADS = 8
 W_PARTS = ((2, 4), (4, 6), (6, 8))
-GROUPS = WIDTHS
-STORES = ((0, 1), (1, 2), (2, 2), (3, 2), (4, 2))
 Y_BANKS = ((4, 5), (6, 7), (0, 1), (4, 5), (6, 7, 2, 3))
 
 
@@ -113,41 +111,41 @@ def tile_list_gelu_kernel(tc, xT, wgt, wt, c, wx_words, wx_scales, b, offs, out)
         x_starts = starts(WIDTHS)
         chunks = len(WIDTHS)
         words = [2 * w for w in WIDTHS]
-        last_rounded = 5 * PIECE
+        last_rounded = J + 2 * PIECE
         region_starts = [last_rounded + 2 * PIECE + s for s in starts(words)]
         arena = sb("arena", [P, region_starts[-1] + words[-1]], F32)
         region = [arena[:, s : s + w] for s, w in zip(region_starts, words)]
         slots = (
-            (PIECE, 2 * PIECE),
-            (3 * PIECE, 4 * PIECE),
-            (0, 2 * PIECE),
-            (3 * PIECE, last_rounded),
-            (3 * PIECE + P, last_rounded + P),
+            (0, J),
+            (PIECE, J + PIECE),
+            (2 * PIECE, J),
+            (J + PIECE, last_rounded),
+            (J + PIECE + P, last_rounded + P),
         )
 
         offsets = keep.tile([P, J // 16], U16, name="offsets")
-        nc.sync.dma_start(offsets[:], offs)
         x_view = xT.rearrange("(p t) s -> p t s", t=PACK)
         x_sb = [sb("x_sb%d" % t, [P, T], F32) for t in range(PACK)]
         c_view = c.rearrange("(p t) j -> p t j", t=PACK)
-        c_raw = {q: sb("c_raw%d" % q, [P, PACK, PIECE], F32)[:] for q in range(2, PIECES)}
-        c_raw[1] = arena[:, region_starts[2] :].rearrange("p (t j) -> p t j", t=PACK)
-
-        c_first = [sb("c_first%d" % h, [P, PACK, P], F32) for h in range(2)]
-
-        def raw_half(q, h):
-            return c_first[h][:] if q == 0 else c_raw[q][:, :, h * P : (h + 1) * P]
+        first_units = starts(C_LOADS)
+        c_raw = [
+            arena[:, region_starts[2] :].rearrange("p (t j) -> p t j", t=PACK)
+            if q == 1
+            else sb("c_raw%d" % q, [P, PACK, units * P], F32)[:]
+            for q, units in enumerate(C_LOADS)
+        ]
+        raw_unit = [c_raw[q][:, :, h * P : (h + 1) * P] for q, units in enumerate(C_LOADS) for h in range(units)]
 
         def load_x(t):
             nc.sync.dma_start(out=x_sb[t][:], in_=x_view[:, t, :])
 
         def load_c(q):
-            nc.sync.dma_start(out=c_raw[q], in_=c_view[:, :, q * PIECE : (q + 1) * PIECE])
+            nc.sync.dma_start(out=c_raw[q], in_=c_view[:, :, first_units[q] * P : (first_units[q] + C_LOADS[q]) * P])
 
         turned = bank(4)
         nc.tensor.transpose(turned[:, 0:P], w_rows[:], ident[:])
-        for h in range(2):
-            nc.sync.dma_start(out=c_first[h][:], in_=c_view[:, :, h * P : (h + 1) * P])
+        load_c(0)
+        nc.sync.dma_start(offsets[:], offs)
         wgt_first = sb("wgt_first", [P, PIECE], F32)
         nc.sync.dma_start(out=wgt_first[:], in_=wgt[:, 0:PIECE])
         load_x(0)
@@ -168,78 +166,76 @@ def tile_list_gelu_kernel(tc, xT, wgt, wt, c, wx_words, wx_scales, b, offs, out)
         load_x(3)
         load_c(3)
 
-        c_back, c_bf, y = {}, {}, {}
+        c_back, y = {}, {}
         first_pair = sb("first_pair", [P, 2 * J + PIECE], F32)
-        rounded = (
-            region[0].bitcast(BF16),
-            first_pair[:, 2 * J - PIECE : 2 * J + PIECE].bitcast(BF16),
-            region[0].bitcast(BF16),
-            arena[:, last_rounded : last_rounded + 2 * PIECE].bitcast(BF16),
-        )
-        for q in range(PIECES):
-            c_bf[q] = (rounded[q][:, 0:BANK], rounded[q][:, BANK:], rounded[q])
         spread = sb("spread", [P, J], F32)
-        c_bf[0] = tuple(spread[:, s : s + PIECE].bitcast(BF16) for s in (0, 3 * P))
-        c_bf[2] = tuple(region[h][:, 0:PIECE].bitcast(BF16) for h in range(2))
+        second_load = first_pair[:, 2 * J - PIECE : 2 * J + PIECE]
+        last_load = arena[:, last_rounded : last_rounded + 2 * PIECE]
+        rounded = [
+            words32.bitcast(BF16)
+            for words32 in (
+                spread[:, 3 * P : 5 * P],
+                second_load[:, 0:PIECE],
+                second_load[:, PIECE:],
+                region[0][:, 0:PIECE],
+                region[1][:, 0:PIECE],
+                sb("rounded5", [P, PIECE], F32)[:],
+                last_load[:, 0:PIECE],
+                last_load[:, PIECE:],
+            )
+        ]
         first_codes, first_scales = mx_tiles("cq", J)
         second = {}
         cr_bf = sb("cr_bf", [P, J * PACK], BF16)
 
-        def come_back(q, h):
-            codes, scales = first_codes, first_scales
-            cols = slice(q * PIECE + h * P, q * PIECE + (h + 1) * P)
-            c_back[q, h] = bank((2 * q + h) % BACK_BANKS)
+        def first_quantise(unit):
+            cols = slice(unit * P, (unit + 1) * P)
+            quantise(first_codes[:, cols], first_scales[:, cols], rounded[unit])
+            c_back[unit] = bank(unit % BACK_BANKS)
             for t in range(PACK):
                 rows = slice(t * P, (t + 1) * P)
                 nc.tensor.matmul_mx(
-                    out=c_back[q, h][:, rows],
+                    out=c_back[unit][:, rows],
                     lhsT=eye_codes[:, rows].bitcast(FP8X4),
                     lhsT_scale=eye_scales[:, rows],
-                    rhs=codes[:, cols].bitcast(FP8X4),
-                    rhs_scale=scales[:, cols],
+                    rhs=first_codes[:, cols].bitcast(FP8X4),
+                    rhs_scale=first_scales[:, cols],
                     start=True,
                     stop=True,
                 )
 
-        def first_quantise(q, h):
-            cols = slice(q * PIECE + h * P, q * PIECE + (h + 1) * P)
-            quantise(first_codes[:, cols], first_scales[:, cols], c_bf[q][h])
-            come_back(q, h)
+        def first_tier(unit):
+            nc.scalar.copy(out=woven(rounded[unit]), in_=planes(raw_unit[unit]))
+            first_quantise(unit)
 
-        def first_tier_half(q, h):
-            nc.scalar.copy(out=woven(c_bf[q][h]), in_=planes(raw_half(q, h)))
-            first_quantise(q, h)
-
-        def leftover(q, h):
+        def leftover(unit):
             nc.vector.tensor_tensor(
-                out=woven(cr_bf[:, (2 * q + h) * BANK : (2 * q + h + 1) * BANK]),
-                in0=planes(raw_half(q, h)),
-                in1=planes(c_back[q, h][:].rearrange("p (t j) -> p t j", t=PACK)),
+                out=woven(cr_bf[:, unit * BANK : (unit + 1) * BANK]),
+                in0=planes(raw_unit[unit]),
+                in1=planes(c_back[unit][:].rearrange("p (t j) -> p t j", t=PACK)),
                 op=SUBTRACT,
             )
 
-        g_starts = starts(GROUPS)
-
         def second_tier(groups, codes=None):
-            s, width = g_starts[groups[0]], sum(GROUPS[g] for g in groups)
+            s, width = x_starts[groups[0]], sum(WIDTHS[g] for g in groups)
             if codes is None:
                 codes = sb("cr%d_codes" % s, [P, width], U32)[:]
             scales = sb("cr%d_scales" % s, [P, width], U8)
             quantise(codes, scales[:], cr_bf[:, PACK * s : PACK * (s + width)])
             for g in groups:
-                cols = slice(g_starts[g] - s, g_starts[g] - s + GROUPS[g])
+                cols = slice(x_starts[g] - s, x_starts[g] - s + WIDTHS[g])
                 second[g] = (codes[:, cols], scales[:, cols])
 
         def sums(group, a):
-            width = GROUPS[group]
+            width = WIDTHS[group]
             g, place = divmod(a, N_TILES // len(Y_BANKS[group]))
             return y[group, g][:, place * width : (place + 1) * width]
 
-        def wx_passes(tier, group, closes=False):
+        def wx_passes(tier, group, closes=False, tiles=range(N_TILES)):
             per_bank = N_TILES // len(Y_BANKS[group])
-            cols = slice(g_starts[group], g_starts[group] + GROUPS[group])
+            cols = slice(x_starts[group], x_starts[group] + WIDTHS[group])
             codes, scales = second[group] if tier else (first_codes[:, cols], first_scales[:, cols])
-            for a in range(N_TILES):
+            for a in tiles:
                 opens = tier == 0 and a % per_bank == 0
                 if opens:
                     y[group, a // per_bank] = bank(Y_BANKS[group][a // per_bank])
@@ -288,36 +284,32 @@ def tile_list_gelu_kernel(tc, xT, wgt, wt, c, wx_words, wx_scales, b, offs, out)
             b0, b1 = W_PARTS[i]
             nc.scalar.copy(out=wgt_rest[:, b0 * P : b1 * P], in_=backs[i][:, 0 : (b1 - b0) * P])
 
-        first_tier_half(0, 0)
-        first_tier_half(0, 1)
+        first_tier(0)
         spread_blocks(2, 4)
         spread_blocks(4, 8)
         for i in range(len(W_PARTS)):
             turn_part(i)
         for i in range(len(W_PARTS)):
             collect_part(i)
-        leftover(0, 0)
-        leftover(0, 1)
+        leftover(0)
 
         gather(0, 0, PIECE, first_pair[:, 0:PIECE])
         for b0, b1 in W_PARTS:
             gather(0, b0 * P, b1 * P, first_pair[:, b0 * P : b1 * P])
         gather(1, 0, PIECE, first_pair[:, J : J + PIECE])
         gather(1, PIECE, J - PIECE, first_pair[:, J + PIECE : 2 * J - PIECE])
-        nc.scalar.copy(out=woven(c_bf[1][2]), in_=planes(c_raw[1]))
-        first_quantise(1, 0)
-        first_quantise(1, 1)
+        nc.scalar.copy(out=woven(second_load.bitcast(BF16)), in_=planes(c_raw[1]))
+        first_quantise(1)
+        first_quantise(2)
         gather(1, J - PIECE, J, first_pair[:, 2 * J - PIECE : 2 * J])
-        first_tier_half(2, 0)
-        leftover(1, 0)
-        first_tier_half(2, 1)
-        leftover(1, 1)
-        leftover(2, 0)
+        for unit in range(1, 4):
+            first_tier(unit + 2)
+            leftover(unit)
+        leftover(4)
         second_tier((0, 1))
-        leftover(2, 1)
-        late_gather(2, 0)
-        late_gather(2, 1)
-        late_gather(2, 2)
+        leftover(5)
+        gather(2, 0, PIECE, arena[:, 0:PIECE])
+        gather(2, PIECE, 3 * PIECE, arena[:, PIECE : 3 * PIECE])
 
         turned_bias = bank(7)
         nc.tensor.transpose(turned_bias[:, 0:P], w_rows[:], ident[:])
@@ -351,10 +343,10 @@ def tile_list_gelu_kernel(tc, xT, wgt, wt, c, wx_words, wx_scales, b, offs, out)
         picks = {}
 
         def project(group, closes=True):
-            width = GROUPS[group]
+            width = WIDTHS[group]
             per_bank = N_TILES // len(Y_BANKS[group])
             codes, scales = picks[group] = mx_tiles("xg%d" % group, width)
-            s = region_starts[0] + 2 * g_starts[group]
+            s = region_starts[0] + 2 * x_starts[group]
             quantise(codes[:], scales[:], arena[:, s : s + 2 * width].bitcast(BF16))
             for a in range(N_TILES):
                 nc.tensor.matmul_mx(
@@ -367,25 +359,20 @@ def tile_list_gelu_kernel(tc, xT, wgt, wt, c, wx_words, wx_scales, b, offs, out)
                     stop=(closes and a % per_bank == per_bank - 1),
                 )
 
-        results = {}
+        def activate(target, group, a):
+            nc.scalar.activation(out=target, in_=sums(group, a), func=GELU, bias=bias[:, a : a + 1])
 
-        def finish(group):
-            first, per_store = STORES[group]
-            j0 = g_starts[first]
-            s, width = g_starts[group] - j0, GROUPS[group]
-            span = sum(w for g, w in enumerate(GROUPS) if STORES[g][0] == first)
-            for a0 in range(0, N_TILES, per_store):
-                if group == first:
-                    results[first, a0] = sb("result%d_%d" % (group, a0), [P, per_store, span], F32)
-                result = results[first, a0]
+        def finish(group, tiles, per_store):
+            j0, width = x_starts[group], WIDTHS[group]
+            for a0 in tiles[::per_store]:
+                result = results[group, a0] = sb("result%d_%d" % (group, a0), [P, per_store, width], F32)
                 for a in range(a0, a0 + per_store):
-                    nc.scalar.activation(
-                        out=result[:, a - a0, s : s + width], in_=sums(group, a), func=GELU, bias=bias[:, a : a + 1]
-                    )
-                if s + width == span:
-                    nc.sync.dma_start(out=out_view[:, a0 : a0 + per_store, j0 : j0 + span], in_=result[:])
+                    activate(result[:, a - a0, :], group, a)
+                nc.sync.dma_start(out=out_view[:, a0 : a0 + per_store, j0 : j0 + width], in_=result[:])
 
-        last = PIECES - 1
+        results = {}
+        every_tile = range(N_TILES)
+
         late_gather(3, 0)
         weave_pair(0, 2, nc.scalar.copy)
         late_gather(3, 1)
@@ -396,31 +383,37 @@ def tile_list_gelu_kernel(tc, xT, wgt, wt, c, wx_words, wx_scales, b, offs, out)
         project(0)
         late_gather(3, 2)
         project(1)
-        nc.scalar.copy(out=woven(c_bf[last][2]), in_=planes(c_raw[last]))
-        finish(0)
-        finish(1)
+        nc.scalar.copy(out=woven(last_load.bitcast(BF16)), in_=planes(c_raw[3]))
+        finish(0, every_tile, 1)
+        finish(1, every_tile, 2)
         weave_pair(2, 2, nc.vector.tensor_copy)
         second_tier((2,), held[:, N:])
         wx_passes(1, 2)
-        first_quantise(last, 0)
-        first_quantise(last, 1)
+        first_quantise(6)
+        first_quantise(7)
         late_gather(2, 3)
         late_gather(2, 4)
         project(2)
-        finish(2)
+        finish(2, every_tile, 2)
         late_gather(3, 3)
         late_gather(3, 4)
         wx_passes(0, 3)
-        leftover(last, 0)
+        leftover(6)
         weave_pair(3, 2, nc.vector.tensor_copy)
         second_tier((3,))
         wx_passes(1, 3)
         weave_pair(4, 2, nc.vector.tensor_copy)
         project(3)
-        finish(3)
-        leftover(last, 1)
+        finish(3, range(0, 2), 2)
+        joint = [sb("joint%d" % a, [P, PIECE], F32) for a in range(2)]
+        for a in range(2):
+            activate(joint[a][:, 0:P], 3, 2 + a)
+        leftover(7)
         wx_passes(0, 4)
         project(4, closes=False)
         second_tier((4,))
-        wx_passes(1, 4, closes=True)
-        finish(4)
+        wx_passes(1, 4, closes=True, tiles=(2, 3, 0, 1))
+        for a in range(2):
+            activate(joint[a][:, P:], 4, 2 + a)
+            nc.sync.dma_start(out=out_view[:, 2 + a, x_starts[3] :], in_=joint[a][:])
+        finish(4, range(0, 2), 1)

@@ -146,8 +146,8 @@ def tile_list_gelu_kernel(tc, xT, wgt, wt, c, wx_words, wx_scales, b, offs, out)
         nc.tensor.transpose(turned[:, 0:P], w_rows[:], ident[:])
         load_c(0)
         nc.sync.dma_start(offsets[:], offs)
-        wgt_first = sb("wgt_first", [P, PIECE], F32)
-        nc.sync.dma_start(out=wgt_first[:], in_=wgt[:, 0:PIECE])
+        wgt_sb = sb("wgt_sb", [P, J], F32)
+        nc.sync.dma_start(out=wgt_sb[:, 0:PIECE], in_=wgt[:, 0:PIECE])
         load_x(0)
         load_x(1)
         nc.sync.dma_start(out=w_rows[P // 2 : P // 2 + N_TILES, :], in_=b.rearrange("(a p) -> a p", p=P))
@@ -253,8 +253,7 @@ def tile_list_gelu_kernel(tc, xT, wgt, wt, c, wx_words, wx_scales, b, offs, out)
             s, width, slot = x_starts[chunk], WIDTHS[chunk], slots[chunk][t - 2]
             gather(t, s, s + width, arena[:, slot : slot + width])
 
-        def gather(t, j0, j1, target):
-            weights = wgt_first if j1 <= PIECE else wgt_rest
+        def gather(t, j0, j1, target, weights=wgt_sb):
             nc.vector.tensor_tensor(
                 out=target,
                 in0=x_sb[t][:].indirect(offsets[:, j0 // 16 : j1 // 16]),
@@ -262,7 +261,6 @@ def tile_list_gelu_kernel(tc, xT, wgt, wt, c, wx_words, wx_scales, b, offs, out)
                 op=MULT,
             )
 
-        wgt_rest = sb("wgt_rest", [P, J], F32)
         by_block = turned[:, 0 : P // 2].rearrange("p (h b) -> p b h", h=HEADS)
         backs = []
 
@@ -282,7 +280,7 @@ def tile_list_gelu_kernel(tc, xT, wgt, wt, c, wx_words, wx_scales, b, offs, out)
 
         def collect_part(i):
             b0, b1 = W_PARTS[i]
-            nc.scalar.copy(out=wgt_rest[:, b0 * P : b1 * P], in_=backs[i][:, 0 : (b1 - b0) * P])
+            nc.scalar.copy(out=wgt_sb[:, b0 * P : b1 * P], in_=backs[i][:, 0 : (b1 - b0) * P])
 
         first_tier(0)
         spread_blocks(2, 4)
@@ -291,13 +289,14 @@ def tile_list_gelu_kernel(tc, xT, wgt, wt, c, wx_words, wx_scales, b, offs, out)
             turn_part(i)
         for i in range(len(W_PARTS)):
             collect_part(i)
+        wgt_first = sb("wgt_first", [P, PIECE], F32)
+        nc.scalar.copy(out=wgt_first[:], in_=wgt_sb[:, 0:PIECE])
         leftover(0)
 
         gather(0, 0, PIECE, first_pair[:, 0:PIECE])
-        for b0, b1 in W_PARTS:
-            gather(0, b0 * P, b1 * P, first_pair[:, b0 * P : b1 * P])
-        gather(1, 0, PIECE, first_pair[:, J : J + PIECE])
-        gather(1, PIECE, J - PIECE, first_pair[:, J + PIECE : 2 * J - PIECE])
+        gather(0, PIECE, 2 * PIECE, first_pair[:, PIECE : 2 * PIECE])
+        gather(0, 2 * PIECE, J, first_pair[:, 2 * PIECE : J])
+        gather(1, 0, J - PIECE, first_pair[:, J : 2 * J - PIECE])
         nc.scalar.copy(out=woven(second_load.bitcast(BF16)), in_=planes(c_raw[1]))
         first_quantise(1)
         first_quantise(2)
@@ -308,8 +307,7 @@ def tile_list_gelu_kernel(tc, xT, wgt, wt, c, wx_words, wx_scales, b, offs, out)
         leftover(4)
         second_tier((0, 1))
         leftover(5)
-        gather(2, 0, PIECE, arena[:, 0:PIECE])
-        gather(2, PIECE, 3 * PIECE, arena[:, PIECE : 3 * PIECE])
+        gather(2, 0, 3 * PIECE, arena[:, 0 : 3 * PIECE])
 
         turned_bias = bank(7)
         nc.tensor.transpose(turned_bias[:, 0:P], w_rows[:], ident[:])
@@ -373,7 +371,7 @@ def tile_list_gelu_kernel(tc, xT, wgt, wt, c, wx_words, wx_scales, b, offs, out)
         results = {}
         every_tile = range(N_TILES)
 
-        late_gather(3, 0)
+        gather(3, 0, PIECE, arena[:, J : J + PIECE], wgt_first)
         weave_pair(0, 2, nc.scalar.copy)
         late_gather(3, 1)
         weave_pair(1, 2, nc.scalar.copy)
@@ -391,12 +389,10 @@ def tile_list_gelu_kernel(tc, xT, wgt, wt, c, wx_words, wx_scales, b, offs, out)
         wx_passes(1, 2)
         first_quantise(6)
         first_quantise(7)
-        late_gather(2, 3)
-        late_gather(2, 4)
+        gather(2, 3 * PIECE, J, arena[:, J + PIECE : J + 2 * PIECE])
         project(2)
         finish(2, every_tile, 2)
-        late_gather(3, 3)
-        late_gather(3, 4)
+        gather(3, 3 * PIECE, J, last_load[:, 0:PIECE])
         wx_passes(0, 3)
         leftover(6)
         weave_pair(3, 2, nc.vector.tensor_copy)

@@ -115,6 +115,7 @@ def tile_list_gelu_kernel(tc, xT, wgt, wt, c, wx_words, wx_scales, b, offs, out)
         region_starts = [last_rounded + 2 * PIECE + s for s in starts(words)]
         arena = sb("arena", [P, region_starts[-1] + words[-1]], F32)
         region = [arena[:, s : s + w] for s, w in zip(region_starts, words)]
+        region[0] = sb("first_woven", [P, words[0]], F32)[:]
         slots = (
             (0, J),
             (PIECE, J + PIECE),
@@ -321,7 +322,7 @@ def tile_list_gelu_kernel(tc, xT, wgt, wt, c, wx_words, wx_scales, b, offs, out)
 
         pairs = first_pair[:, 0 : 2 * J].rearrange("p (t j) -> p t j", t=2)
 
-        def weave_pair(chunk, t0, copy):
+        def weave_pair(chunk, t0, copy, cols=slice(None)):
             s, width = x_starts[chunk], WIDTHS[chunk]
             if t0 == 0:
                 source = pairs[:, :, s : s + width]
@@ -329,27 +330,36 @@ def tile_list_gelu_kernel(tc, xT, wgt, wt, c, wx_words, wx_scales, b, offs, out)
                 first, second = (slot // width for slot in slots[chunk])
                 source = arena[:].rearrange("p (u j) -> p u j", j=width)[:, first : second + 1 : second - first, :]
             target = region[chunk].bitcast(BF16).rearrange("p (j t) -> p j t", t=PACK)
-            copy(out=target[:, :, t0 : t0 + 2], in_=source.rearrange("p t j -> p j t"))
+            copy(out=target[:, cols, t0 : t0 + 2], in_=source.rearrange("p t j -> p j t")[:, cols, :])
 
         for chunk in range(chunks):
             weave_pair(chunk, 0, nc.scalar.copy)
 
         wt_bf = sb("wt_bf", [P, N * PACK], BF16)
         nc.scalar.copy(out=woven(wt_bf[:]), in_=planes(wt_raw[:]))
+        wt_scales = sb("wt_scales", [P, N], U8)
+        wt_codes = []
+
+        def quantise_wt(codes):
+            cols = slice(len(wt_codes) * PIECE, (len(wt_codes) + 1) * PIECE)
+            wt_codes.append(codes)
+            quantise(codes, wt_scales[:, cols], wt_bf[:, PACK * cols.start : PACK * cols.stop])
 
         out_view = out.rearrange("(a p) j -> p a j", p=P)
         picks = {}
 
-        def project(group, closes=True):
-            width = WIDTHS[group]
+        def project(group, closes=True, tiles=range(N_TILES)):
+            codes, scales = picks[group] = mx_tiles("xg%d" % group, WIDTHS[group])
+            quantise(codes[:], scales[:], region[group].bitcast(BF16))
+            multiply(group, tiles, closes)
+
+        def multiply(group, tiles, closes=True):
             per_bank = N_TILES // len(Y_BANKS[group])
-            codes, scales = picks[group] = mx_tiles("xg%d" % group, width)
-            s = region_starts[0] + 2 * x_starts[group]
-            quantise(codes[:], scales[:], arena[:, s : s + 2 * width].bitcast(BF16))
-            for a in range(N_TILES):
+            codes, scales = picks[group]
+            for a in tiles:
                 nc.tensor.matmul_mx(
                     out=sums(group, a),
-                    lhsT=wt_codes[:, a * P : (a + 1) * P].bitcast(FP8X4),
+                    lhsT=wt_codes[a // 2][:, a % 2 * P : (a % 2 + 1) * P].bitcast(FP8X4),
                     lhsT_scale=wt_scales[:, a * P : (a + 1) * P],
                     rhs=codes[:].bitcast(FP8X4),
                     rhs_scale=scales[:],
@@ -371,21 +381,26 @@ def tile_list_gelu_kernel(tc, xT, wgt, wt, c, wx_words, wx_scales, b, offs, out)
         results = {}
         every_tile = range(N_TILES)
 
-        gather(3, 0, PIECE, arena[:, J : J + PIECE], wgt_first)
-        weave_pair(0, 2, nc.scalar.copy)
-        late_gather(3, 1)
-        weave_pair(1, 2, nc.scalar.copy)
-        held = sb("wgt_first", [P, N + PIECE], U32)
-        wt_codes, wt_scales = held[:, 0:N], sb("wt_scales", [P, N], U8)
-        quantise(wt_codes, wt_scales[:], wt_bf[:])
-        project(0)
+        def early_half(s, weights):
+            gather(3, s, s + P, arena[:, J + s : J + s + P], weights)
+            weave_pair(s // PIECE, 2, nc.scalar.copy, slice(s % PIECE, s % PIECE + P))
+
+        early_half(0, wgt_first)
+        early_half(P, wgt_first)
+        early_half(2 * P, wgt_sb)
+        early_half(3 * P, wgt_sb)
+        quantise_wt(sb("wgt_first", [P, PIECE], U32)[:])
+        project(0, tiles=range(0, 2))
         late_gather(3, 2)
+        held = sb("first_woven", [P, 2 * PIECE], U32)
+        quantise_wt(held[:, 0:PIECE])
+        multiply(0, range(2, 4))
         project(1)
         nc.scalar.copy(out=woven(last_load.bitcast(BF16)), in_=planes(c_raw[3]))
         finish(0, every_tile, 1)
         finish(1, every_tile, 2)
         weave_pair(2, 2, nc.vector.tensor_copy)
-        second_tier((2,), held[:, N:])
+        second_tier((2,), held[:, PIECE:])
         wx_passes(1, 2)
         first_quantise(6)
         first_quantise(7)

@@ -205,8 +205,8 @@ def tile_list_gelu_kernel(tc, xT, wgt, wt, c, wx_words, wx_scales, b, offs, out)
                     stop=True,
                 )
 
-        def first_tier(unit):
-            nc.scalar.copy(out=woven(rounded[unit]), in_=planes(raw_unit[unit]))
+        def first_tier(unit, copy=nc.scalar.copy):
+            copy(out=woven(rounded[unit]), in_=planes(raw_unit[unit]))
             first_quantise(unit)
 
         def leftover(unit):
@@ -302,8 +302,8 @@ def tile_list_gelu_kernel(tc, xT, wgt, wt, c, wx_words, wx_scales, b, offs, out)
         first_quantise(1)
         first_quantise(2)
         gather(1, J - PIECE, J, first_pair[:, 2 * J - PIECE : 2 * J])
-        for unit in range(1, 4):
-            first_tier(unit + 2)
+        for unit, copy in zip(range(1, 4), (nc.scalar.copy, nc.scalar.copy, nc.vector.tensor_copy)):
+            first_tier(unit + 2, copy)
             leftover(unit)
         leftover(4)
         second_tier((0, 1))

@@ -309,16 +309,16 @@ def tile_list_gelu_kernel(tc, xT, wgt, wt, c, wx_words, wx_scales, b, offs, out)
         second_tier((0, 1))
         leftover(5)
         gather(2, 0, 3 * PIECE, arena[:, 0 : 3 * PIECE])
+        second_tier((2,))
 
         turned_bias = bank(7)
         nc.tensor.transpose(turned_bias[:, 0:P], w_rows[:], ident[:])
         bias = sb("bias", [P, N_TILES], F32)
         nc.scalar.copy(out=bias[:], in_=turned_bias[:, P // 2 : P // 2 + N_TILES])
 
-        for group in range(2):
+        for group in range(3):
             wx_passes(0, group)
             wx_passes(1, group)
-        wx_passes(0, 2)
 
         pairs = first_pair[:, 0 : 2 * J].rearrange("p (t j) -> p t j", t=2)
 
@@ -392,16 +392,14 @@ def tile_list_gelu_kernel(tc, xT, wgt, wt, c, wx_words, wx_scales, b, offs, out)
         quantise_wt(sb("wgt_first", [P, PIECE], U32)[:])
         project(0, tiles=range(0, 2))
         late_gather(3, 2)
-        held = sb("first_woven", [P, 2 * PIECE], U32)
-        quantise_wt(held[:, 0:PIECE])
+        quantise_wt(sb("first_woven", [P, PIECE], U32)[:])
         multiply(0, range(2, 4))
         project(1)
-        nc.scalar.copy(out=woven(last_load.bitcast(BF16)), in_=planes(c_raw[3]))
+        nc.scalar.copy(out=woven(rounded[6]), in_=planes(raw_unit[6]))
+        nc.vector.tensor_copy(out=woven(rounded[7]), in_=planes(raw_unit[7]))
         finish(0, every_tile, 1)
         finish(1, every_tile, 2)
         weave_pair(2, 2, nc.vector.tensor_copy)
-        second_tier((2,), held[:, PIECE:])
-        wx_passes(1, 2)
         first_quantise(6)
         first_quantise(7)
         gather(2, 3 * PIECE, J, arena[:, J + PIECE : J + 2 * PIECE])

@@ -395,8 +395,7 @@ def tile_list_gelu_kernel(tc, xT, wgt, wt, c, wx_words, wx_scales, b, offs, out)
         quantise_wt(sb("first_woven", [P, PIECE], U32)[:])
         multiply(0, range(2, 4))
         project(1)
-        nc.scalar.copy(out=woven(rounded[6]), in_=planes(raw_unit[6]))
-        nc.vector.tensor_copy(out=woven(rounded[7]), in_=planes(raw_unit[7]))
+        nc.scalar.copy(out=woven(last_load.bitcast(BF16)), in_=planes(c_raw[3]))
         finish(0, every_tile, 1)
         finish(1, every_tile, 2)
         weave_pair(2, 2, nc.vector.tensor_copy)

from contextlib import ExitStack

import concourse.mybir as mybir

K, L, N, T, J = 512, 512, 512, 2048, 1024
FLOPS = 2 * N * J * (K + 2 * L) + 2 * L * L * J

F32 = mybir.dt.float32
BF16 = mybir.dt.bfloat16
I32 = mybir.dt.int32
U32 = mybir.dt.uint32
U16 = mybir.dt.uint16
U8 = mybir.dt.uint8
FP8X4 = mybir.dt.float8_e4m3fn_x4
FP4X4 = mybir.dt.float4_e2m1fn_x4
MULT = mybir.AluOpType.mult
SUBTRACT = mybir.AluOpType.subtract
ADD = mybir.AluOpType.add
IS_EQUAL = mybir.AluOpType.is_equal
GELU = mybir.ActivationFunctionType.Gelu_apprx_tanh

P = 128
PACK = 4
QUAD = 32
N_TILES = N // P
BANK = 512
PIECE = 256
C_LOADS = (1, 2, 3, 2)
BACK_BANKS = 4
WIDTHS = (256, 256, 256, 128, 128)
HEADS = 8
W_PARTS = ((2, 4), (4, 6), (6, 8))
Y_BANKS = ((4, 5), (6, 7), (0, 1), (4, 5), (6, 7, 2, 3))


def starts(widths):
    return [sum(widths[:i]) for i in range(len(widths))]


def woven(tile):
    return tile.rearrange("p (c i t) -> p c t i", i=4, t=PACK)


def planes(tile):
    return tile.rearrange("p t (c i) -> p c t i", i=4)


def tile_list_gelu_kernel(tc, xT, wgt, wt, c, wx_words, wx_scales, b, offs, out):
    nc = tc.nc
    with ExitStack() as ctx:
        keep = ctx.enter_context(tc.tile_pool(name="keep", bufs=1))
        psum = ctx.enter_context(tc.psum_pool(name="psum", bufs=1))

        def sb(name, shape, dtype):
            return keep.tile(shape, dtype, name=name, align_bytes=64)

        def bank(number):
            return psum.tile([P, BANK], F32, name="bank%d" % number)

        def quantise(codes, scales, values):
            nc.vector.quantize_mx(out=codes.bitcast(FP8X4), scales=scales, in_=values)

        def mx_tiles(name, width):
            return sb(name + "_codes", [P, width], U32), sb(name + "_scales", [P, width], U8)

        w_rows = sb("w_rows", [P, P], F32)
        nc.scalar.dma_start(
            out=w_rows[0 : P // 2, :], in_=wgt[0 : P : P // HEADS, :].rearrange("h (b j) -> h b j", j=P)
        )
        base = sb("base", [P, 1], F32)
        for quad in range(P // QUAD):
            nc.gpsimd.memset(base[QUAD * quad : QUAD * (quad + 1), :], float(QUAD * quad))
        nc.gpsimd.memset(w_rows[P // 2 :, :], 0.0)
        ones = sb("ones", [P, P], F32)
        nc.vector.memset(ones[:], 1.0)
        warm = sb("warm", [P, 2], F32)
        nc.scalar.activation(out=warm[:], in_=ones[:, 0:2], func=GELU)
        wx_plane = sb("wx_plane", [P, N], U8)
        nc.vector.memset(wx_plane[:].bitcast(U32), 0)

        def count(name, width):
            counted = sb(name, [P, width], F32)
            nc.vector.tensor_tensor_scan(
                out=counted[:], data0=ones[:, 0:width], data1=ones[:, 0:width], initial=0.0, op0=MULT, op1=ADD
            )
            return counted

        short = count("short", QUAD)
        column = count("column", P)
        row = sb("row", [P, QUAD], F32)
        nc.vector.transpose(out=row[:], in_=short[:])

        def diagonal(target, places):
            nc.vector.tensor_scalar(
                out=target, in0=places, scalar1=base[:], scalar2=row[:, 0:1], op0=SUBTRACT, op1=IS_EQUAL
            )

        eye = [sb("eye%d" % u, [P, 2 * (BANK + 1)], BF16) for u in range(2)]
        ident = sb("ident", [P, P], F32)
        nc.vector.memset(eye[0][:, 0 : 2 * BANK].bitcast(U32), 0)
        diagonal(ident[:], column[:])
        nc.vector.memset(eye[1][:, 0 : 2 * BANK].bitcast(U32), 0)
        eye_codes, eye_scales = mx_tiles("eye", PACK * P)
        for u in range(2):
            diagonals = eye[u][:].rearrange("p (j r) -> p j r", j=2)
            diagonal(diagonals[:, :, 2 * u : 2 * u + BANK - 2 : PACK], column[:].unsqueeze(1).to_broadcast([P, 2, P]))
        for u in range(2):
            half = slice(u * PIECE, (u + 1) * PIECE)
            quantise(eye_codes[:, half], eye_scales[:, half], eye[u][:, 0 : 2 * BANK])

        x_starts = starts(WIDTHS)
        chunks = len(WIDTHS)
        words = [2 * w for w in WIDTHS]
        last_rounded = J + 2 * PIECE
        region_starts = [last_rounded + 2 * PIECE + s for s in starts(words)]
        arena = sb("arena", [P, region_starts[-1] + words[-1]], F32)
        region = [arena[:, s : s + w] for s, w in zip(region_starts, words)]
        region[0] = sb("first_woven", [P, words[0]], F32)[:]
        slots = (
            (0, J),
            (PIECE, J + PIECE),
            (2 * PIECE, J),
            (J + PIECE, last_rounded),
            (J + PIECE + P, last_rounded + P),
        )

        offsets = keep.tile([P, J // 16], U16, name="offsets")
        x_view = xT.rearrange("(p t) s -> p t s", t=PACK)
        x_sb = [sb("x_sb%d" % t, [P, T], F32) for t in range(PACK)]
        c_view = c.rearrange("(p t) j -> p t j", t=PACK)
        first_units = starts(C_LOADS)
        c_raw = [
            arena[:, region_starts[2] :].rearrange("p (t j) -> p t j", t=PACK)
            if q == 1
            else sb("c_raw%d" % q, [P, PACK, units * P], F32)[:]
            for q, units in enumerate(C_LOADS)
        ]
        raw_unit = [c_raw[q][:, :, h * P : (h + 1) * P] for q, units in enumerate(C_LOADS) for h in range(units)]

        def load_x(t):
            nc.sync.dma_start(out=x_sb[t][:], in_=x_view[:, t, :])

        def load_c(q):
            nc.sync.dma_start(out=c_raw[q], in_=c_view[:, :, first_units[q] * P : (first_units[q] + C_LOADS[q]) * P])

        turned = bank(4)
        nc.tensor.transpose(turned[:, 0:P], w_rows[:], ident[:])
        load_c(0)
        nc.sync.dma_start(offsets[:], offs)
        wgt_sb = sb("wgt_sb", [P, J], F32)
        nc.sync.dma_start(out=wgt_sb[:, 0:PIECE], in_=wgt[:, 0:PIECE])
        load_x(0)
        load_x(1)
        nc.sync.dma_start(out=w_rows[P // 2 : P // 2 + N_TILES, :], in_=b.rearrange("(a p) -> a p", p=P))
        load_c(1)
        load_c(2)
        load_x(2)
        wx_sb = sb("wx_sb", [P, 2 * N], U8)
        nc.sync.dma_start(out=wx_sb[:].bitcast(I32), in_=wx_words[0].bitcast(I32))
        for quad in range(4):
            nc.sync.dma_start(
                out=wx_plane[32 * quad : 32 * quad + 4, :].bitcast(I32),
                in_=wx_scales[0, 4 * quad : 4 * quad + 4, :].bitcast(I32),
            )
        wt_raw = sb("wt_raw", [P, PACK, N], F32)
        nc.sync.dma_start(out=wt_raw[:], in_=wt.rearrange("(p t) n -> p t n", t=PACK))
        load_x(3)
        load_c(3)

        c_back, y = {}, {}
        first_pair = sb("first_pair", [P, 2 * J + PIECE], F32)
        spread = sb("spread", [P, J], F32)
        second_load = first_pair[:, 2 * J - PIECE : 2 * J + PIECE]
        last_load = arena[:, last_rounded : last_rounded + 2 * PIECE]
        rounded = [
            words32.bitcast(BF16)
            for words32 in (
                spread[:, 3 * P : 5 * P],
                second_load[:, 0:PIECE],
                second_load[:, PIECE:],
                region[0][:, 0:PIECE],
                region[1][:, 0:PIECE],
                sb("rounded5", [P, PIECE], F32)[:],
                last_load[:, 0:PIECE],
                last_load[:, PIECE:],
            )
        ]
        first_codes, first_scales = mx_tiles("cq", J)
        second = {}
        cr_bf = sb("cr_bf", [P, J * PACK], BF16)

        def first_quantise(unit):
            cols = slice(unit * P, (unit + 1) * P)
            quantise(first_codes[:, cols], first_scales[:, cols], rounded[unit])
            c_back[unit] = bank(unit % BACK_BANKS)
            for t in range(PACK):
                rows = slice(t * P, (t + 1) * P)
                nc.tensor.matmul_mx(
                    out=c_back[unit][:, rows],
                    lhsT=eye_codes[:, rows].bitcast(FP8X4),
                    lhsT_scale=eye_scales[:, rows],
                    rhs=first_codes[:, cols].bitcast(FP8X4),
                    rhs_scale=first_scales[:, cols],
                    start=True,
                    stop=True,
                )

        def first_tier(unit, copy=nc.scalar.copy):
            copy(out=woven(rounded[unit]), in_=planes(raw_unit[unit]))
            first_quantise(unit)

        def leftover(unit):
            nc.vector.tensor_tensor(
                out=woven(cr_bf[:, unit * BANK : (unit + 1) * BANK]),
                in0=planes(raw_unit[unit]),
                in1=planes(c_back[unit][:].rearrange("p (t j) -> p t j", t=PACK)),
                op=SUBTRACT,
            )

        def second_tier(groups, codes=None):
            s, width = x_starts[groups[0]], sum(WIDTHS[g] for g in groups)
            if codes is None:
                codes = sb("cr%d_codes" % s, [P, width], U32)[:]
            scales = sb("cr%d_scales" % s, [P, width], U8)
            quantise(codes, scales[:], cr_bf[:, PACK * s : PACK * (s + width)])
            for g in groups:
                cols = slice(x_starts[g] - s, x_starts[g] - s + WIDTHS[g])
                second[g] = (codes[:, cols], scales[:, cols])

        def sums(group, a):
            width = WIDTHS[group]
            g, place = divmod(a, N_TILES // len(Y_BANKS[group]))
            return y[group, g][:, place * width : (place + 1) * width]

        def wx_passes(tier, group, closes=False, tiles=range(N_TILES)):
            per_bank = N_TILES // len(Y_BANKS[group])
            cols = slice(x_starts[group], x_starts[group] + WIDTHS[group])
            codes, scales = second[group] if tier else (first_codes[:, cols], first_scales[:, cols])
            for a in tiles:
                opens = tier == 0 and a % per_bank == 0
                if opens:
                    y[group, a // per_bank] = bank(Y_BANKS[group][a // per_bank])
                nc.tensor.matmul_mx(
                    out=sums(group, a),
                    lhsT=wx_sb[:, 2 * a * P : 2 * (a + 1) * P].bitcast(FP4X4),
                    lhsT_scale=wx_plane[:, a * P : (a + 1) * P],
                    rhs=codes.bitcast(FP8X4),
                    rhs_scale=scales,
                    start=opens,
                    stop=(closes and a % per_bank == per_bank - 1),
                )

        def late_gather(t, chunk):
            s, width, slot = x_starts[chunk], WIDTHS[chunk], slots[chunk][t - 2]
            gather(t, s, s + width, arena[:, slot : slot + width])

        def gather(t, j0, j1, target, weights=wgt_sb):
            nc.vector.tensor_tensor(
                out=target,
                in0=x_sb[t][:].indirect(offsets[:, j0 // 16 : j1 // 16]),
                in1=weights[:, j0:j1],
                op=MULT,
            )

        by_block = turned[:, 0 : P // 2].rearrange("p (h b) -> p b h", h=HEADS)
        backs = []

        def spread_blocks(b0, b1):
            nc.scalar.copy(
                out=spread[:, b0 * P : b1 * P].rearrange("p (b h r) -> p b h r", h=HEADS, r=P // HEADS),
                in_=by_block[:, b0:b1, :].unsqueeze(3).to_broadcast([P, b1 - b0, HEADS, P // HEADS]),
            )

        def turn_part(i):
            b0, b1 = W_PARTS[i]
            backs.append(bank(5 + i))
            for blk in range(b0, b1):
                nc.tensor.transpose(
                    backs[i][:, (blk - b0) * P : (blk - b0 + 1) * P], spread[:, blk * P : (blk + 1) * P], ident[:]
                )

        def collect_part(i):
            b0, b1 = W_PARTS[i]
            nc.scalar.copy(out=wgt_sb[:, b0 * P : b1 * P], in_=backs[i][:, 0 : (b1 - b0) * P])

        first_tier(0)
        spread_blocks(2, 4)
        spread_blocks(4, 8)
        for i in range(len(W_PARTS)):
            turn_part(i)
        for i in range(len(W_PARTS)):
            collect_part(i)
        wgt_first = sb("wgt_first", [P, PIECE], F32)
        nc.scalar.copy(out=wgt_first[:], in_=wgt_sb[:, 0:PIECE])
        leftover(0)

        gather(0, 0, PIECE, first_pair[:, 0:PIECE])
        gather(0, PIECE, 2 * PIECE, first_pair[:, PIECE : 2 * PIECE])
        gather(0, 2 * PIECE, J, first_pair[:, 2 * PIECE : J])
        gather(1, 0, J - PIECE, first_pair[:, J : 2 * J - PIECE])
        nc.scalar.copy(out=woven(second_load.bitcast(BF16)), in_=planes(c_raw[1]))
        first_quantise(1)
        first_quantise(2)
        gather(1, J - PIECE, J, first_pair[:, 2 * J - PIECE : 2 * J])
        for unit, copy in zip(range(1, 4), (nc.scalar.copy, nc.scalar.copy, nc.vector.tensor_copy)):
            first_tier(unit + 2, copy)
            leftover(unit)
        leftover(4)
        second_tier((0, 1))
        leftover(5)
        gather(2, 0, 3 * PIECE, arena[:, 0 : 3 * PIECE])
        second_tier((2,))

        turned_bias = bank(7)
        nc.tensor.transpose(turned_bias[:, 0:P], w_rows[:], ident[:])
        bias = sb("bias", [P, N_TILES], F32)
        nc.scalar.copy(out=bias[:], in_=turned_bias[:, P // 2 : P // 2 + N_TILES])

        for group in range(3):
            wx_passes(0, group)
            wx_passes(1, group)

        pairs = first_pair[:, 0 : 2 * J].rearrange("p (t j) -> p t j", t=2)

        def weave_pair(chunk, t0, copy, cols=slice(None)):
            s, width = x_starts[chunk], WIDTHS[chunk]
            if t0 == 0:
                source = pairs[:, :, s : s + width]
            else:
                first, second = (slot // width for slot in slots[chunk])
                source = arena[:].rearrange("p (u j) -> p u j", j=width)[:, first : second + 1 : second - first, :]
            target = region[chunk].bitcast(BF16).rearrange("p (j t) -> p j t", t=PACK)
            copy(out=target[:, cols, t0 : t0 + 2], in_=source.rearrange("p t j -> p j t")[:, cols, :])

        for chunk in range(chunks):
            weave_pair(chunk, 0, nc.scalar.copy)

        wt_bf = sb("wt_bf", [P, N * PACK], BF16)
        nc.scalar.copy(out=woven(wt_bf[:]), in_=planes(wt_raw[:]))
        wt_scales = sb("wt_scales", [P, N], U8)
        wt_codes = []

        def quantise_wt(codes):
            cols = slice(len(wt_codes) * PIECE, (len(wt_codes) + 1) * PIECE)
            wt_codes.append(codes)
            quantise(codes, wt_scales[:, cols], wt_bf[:, PACK * cols.start : PACK * cols.stop])

        out_view = out.rearrange("(a p) j -> p a j", p=P)
        picks = {}

        def project(group, closes=True, tiles=range(N_TILES)):
            codes, scales = picks[group] = mx_tiles("xg%d" % group, WIDTHS[group])
            quantise(codes[:], scales[:], region[group].bitcast(BF16))
            multiply(group, tiles, closes)

        def multiply(group, tiles, closes=True):
            per_bank = N_TILES // len(Y_BANKS[group])
            codes, scales = picks[group]
            for a in tiles:
                nc.tensor.matmul_mx(
                    out=sums(group, a),
                    lhsT=wt_codes[a // 2][:, a % 2 * P : (a % 2 + 1) * P].bitcast(FP8X4),
                    lhsT_scale=wt_scales[:, a * P : (a + 1) * P],
                    rhs=codes[:].bitcast(FP8X4),
                    rhs_scale=scales[:],
                    start=False,
                    stop=(closes and a % per_bank == per_bank - 1),
                )

        def activate(target, group, a):
            nc.scalar.activation(out=target, in_=sums(group, a), func=GELU, bias=bias[:, a : a + 1])

        def finish(group, tiles, per_store):
            j0, width = x_starts[group], WIDTHS[group]
            for a0 in tiles[::per_store]:
                result = results[group, a0] = sb("result%d_%d" % (group, a0), [P, per_store, width], F32)
                for a in range(a0, a0 + per_store):
                    activate(result[:, a - a0, :], group, a)
                nc.sync.dma_start(out=out_view[:, a0 : a0 + per_store, j0 : j0 + width], in_=result[:])

        results = {}
        every_tile = range(N_TILES)

        def early_half(s, weights):
            gather(3, s, s + P, arena[:, J + s : J + s + P], weights)
            weave_pair(s // PIECE, 2, nc.scalar.copy, slice(s % PIECE, s % PIECE + P))

        early_half(0, wgt_first)
        early_half(P, wgt_first)
        early_half(2 * P, wgt_sb)
        early_half(3 * P, wgt_sb)
        quantise_wt(sb("wgt_first", [P, PIECE], U32)[:])
        project(0, tiles=range(0, 2))
        late_gather(3, 2)
        quantise_wt(sb("first_woven", [P, PIECE], U32)[:])
        multiply(0, range(2, 4))
        project(1)
        nc.scalar.copy(out=woven(last_load.bitcast(BF16)), in_=planes(c_raw[3]))
        finish(0, every_tile, 1)
        finish(1, every_tile, 2)
        weave_pair(2, 2, nc.vector.tensor_copy)
        first_quantise(6)
        first_quantise(7)
        gather(2, 3 * PIECE, J, arena[:, J + PIECE : J + 2 * PIECE])
        project(2)
        finish(2, every_tile, 2)
        gather(3, 3 * PIECE, J, last_load[:, 0:PIECE])
        wx_passes(0, 3)
        leftover(6)
        weave_pair(3, 2, nc.vector.tensor_copy)
        second_tier((3,))
        wx_passes(1, 3)
        weave_pair(4, 2, nc.vector.tensor_copy)
        project(3)
        finish(3, range(0, 2), 2)
        joint = [sb("joint%d" % a, [P, PIECE], F32) for a in range(2)]
        for a in range(2):
            activate(joint[a][:, 0:P], 3, 2 + a)
        leftover(7)
        wx_passes(0, 4)
        project(4, closes=False)
        second_tier((4,))
        wx_passes(1, 4, closes=True, tiles=(2, 3, 0, 1))
        for a in range(2):
            activate(joint[a][:, P:], 4, 2 + a)
            nc.sync.dma_start(out=out_view[:, 2 + a, x_starts[3] :], in_=joint[a][:])
        finish(4, range(0, 2), 1)
